import numpy as np
import ml_dtypes


def mxq(x, axis, fmt="e4m3"):
    dtype, down = {"e4m3": (ml_dtypes.float8_e4m3fn, 7), "e5m2": (ml_dtypes.float8_e5m2, 14)}[fmt]
    v = np.moveaxis(np.asarray(x, np.float32).astype(ml_dtypes.bfloat16).astype(np.float64), axis, -1)
    blocks = v.reshape(v.shape[:-1] + (-1, 32))
    amax = np.abs(blocks).max(-1, keepdims=True)
    byte = np.maximum(np.where(amax > 0, np.frexp(amax)[1] - 1 + 127, 0) - down, 1)
    scale = np.exp2(byte - 127.0)
    codes = (blocks / scale).astype(np.float32).astype(dtype).astype(np.float64)
    return np.moveaxis((codes * scale).reshape(v.shape), -1, axis)


WIDE = False


def mx_kscale(k):
    if not WIDE:
        return np.ones(k)
    levels = np.array([10, -10, 5, -5, 0])
    if k % 512:
        return np.exp2(np.random.permutation(np.resize(levels, k // 32))).repeat(32)
    a = np.empty((k // 512, 16))
    for p in range(k // 512):
        a[p, :8] = np.random.permutation(np.resize(levels, 8))
        for g in range(8):
            far = levels[np.abs(levels - a[p, g]) >= 10]
            a[p, g + 8] = far[np.random.randint(len(far))]
    return np.exp2(a.ravel()).repeat(32)


def f64(x):
    return np.asarray(x).astype(np.float64)


def striped(idx):
    return np.tile(idx.reshape(-1, 16).T, (8, 1)).astype(np.uint16)


def unstriped(offs):
    return offs[:16].T.reshape(-1).astype(np.int64)


E2M1 = np.array([0.0, 0.5, 1.0, 1.5, 2.0, 3.0, 4.0, 6.0, -0.0, -0.5, -1.0, -1.5, -2.0, -3.0, -4.0, -6.0])


def pack_weight(w, fmt):
    k, n = w.shape
    w = f64(np.asarray(w, np.float32).astype(ml_dtypes.bfloat16)).reshape(k // 32, 32, n)
    amax = np.abs(w).max(1)
    if fmt == "e4m3":
        byte = np.frexp(amax)[1] - 1 + 127 - 7
    else:
        mant, ex = np.frexp(amax / 6.0)
        byte = np.where(mant > 0.5, ex, ex - 1) + 127
    byte = np.clip(np.where(amax > 0, byte, 1), 1, 254)
    scaled = (w * np.exp2(127.0 - byte)[:, None, :]).reshape(k, n).astype(np.float32)
    by_word = np.ascontiguousarray(scaled.reshape(k // 512, 128, 4, n).transpose(0, 1, 3, 2))
    if fmt == "e4m3":
        words = by_word.astype(ml_dtypes.float8_e4m3fn).view(np.uint8)
    else:
        c = by_word.astype(ml_dtypes.float4_e2m1fn).view(np.uint8) & 0xF
        words = (c[..., 0::2] | (c[..., 1::2] << 4)).reshape(k // 512, 128, 2 * n)
    return np.ascontiguousarray(words), np.ascontiguousarray(byte.astype(np.uint8).reshape(k // 512, 16, n))


def unpack_weight(words, scales, fmt):
    g, _, n = scales.shape
    words = np.ascontiguousarray(words).reshape(g, 128, n, -1)
    if fmt == "e4m3":
        vals = words.view(ml_dtypes.float8_e4m3fn).astype(np.float64)
    else:
        nib = np.empty((g, 128, n, 4), np.uint8)
        nib[..., 0::2] = words & 0xF
        nib[..., 1::2] = words >> 4
        vals = E2M1[nib]
    vals = vals * np.repeat(np.exp2(scales.astype(np.float64) - 127.0), 8, axis=1)[..., None]
    return vals.transpose(0, 1, 3, 2).reshape(g * 512, n)


def gelu(v):
    return 0.5 * v * (1.0 + np.tanh(np.sqrt(2.0 / np.pi) * (v + 0.044715 * v**3)))


K, T, E, C, N = 1024, 640, 2, 256, 128
K8 = 512


def by_expert(wq, xq):
    return np.concatenate([wq[e].T @ xq[:, e * C:(e + 1) * C] for e in range(E)], axis=1)


def setup_inputs():
    n = np.random.standard_normal
    s = mx_kscale(K)[:, None]
    w = n((E, K, N)) / np.sqrt(K) / s[None]
    w8 = [pack_weight(m[:K8], "e4m3") for m in w]
    w4 = [pack_weight(m[K8:], "e2m1") for m in w]
    return {
        "xT": (n((K, T)) * s).astype(np.float32),
        "w8_words": np.stack([m[0] for m in w8]),
        "w8_scales": np.stack([m[1] for m in w8]),
        "w4_words": np.stack([m[0] for m in w4]),
        "w4_scales": np.stack([m[1] for m in w4]),
        "b": (0.3 * n((N, E))).astype(np.float32),
        "gate": np.tile(np.random.uniform(0.2, 1.0, E * C), (N, 1)).astype(np.float32),
        "offs": striped(np.random.permutation(T)[:E * C]),
        "dst": striped(np.random.permutation(T)[:E * C]),
    }


def reference(xT, w8_words, w8_scales, w4_words, w4_scales, b, gate, offs, dst):
    idx = unstriped(offs)
    w = np.stack([np.concatenate([unpack_weight(w8_words[e], w8_scales[e], "e4m3"), unpack_weight(w4_words[e], w4_scales[e], "e2m1")]) for e in range(E)])
    xq = mxq(f64(xT)[:, idx], 0, "e4m3")
    y = by_expert(w, xq)
    y = gelu(y + np.repeat(f64(b), C, axis=1))
    out = np.zeros((N, T))
    out[:, unstriped(dst)] = f64(gate) * y
    return out

@@ -1,0 +1,126 @@
+import concourse.mybir as mybir
+
+E, K, N, T, C = 2, 1024, 128, 640, 256
+FLOPS = 2 * K * N * E * C
+
+F32 = mybir.dt.float32
+BF16 = mybir.dt.bfloat16
+I32 = mybir.dt.int32
+U32 = mybir.dt.uint32
+U16 = mybir.dt.uint16
+U8 = mybir.dt.uint8
+FP8X4 = mybir.dt.float8_e4m3fn_x4
+FP4X4 = mybir.dt.float4_e2m1fn_x4
+ACT = mybir.ActivationFunctionType
+MULT = mybir.AluOpType.mult
+
+P = 128
+CHUNKS = {
+    0: [(0, 384), (384, 640)],
+    1: [(0, 384), (384, 640)],
+}
+PLANE = [4, 0]
+
+
+def tile_moe_two_lin_gelu_kernel(
+    tc, xT, w8_words, w8_scales, w4_words, w4_scales, b, gate, offs, dst, out
+):
+    nc = tc.nc
+    with (
+        tc.tile_pool(name="keep", bufs=1) as keep,
+        tc.psum_pool(name="psum", bufs=1) as psum,
+    ):
+        offs_t = keep.tile([P, E * C // 16], U16, name="offs_t")
+        dst_t = keep.tile([P, E * C // 16], U16, name="dst_t")
+        x_t = [[keep.tile([P, 4, e - s], F32, name=f"x{a}{i}", align_bytes=64) for i, (s, e) in enumerate(CHUNKS[a])] for a in range(2)]
+        xb = [keep.tile([P, T, 4], BF16, name=f"xb{a}", align_bytes=64) for a in range(2)]
+        words = [keep.tile([P, T], U32, name=f"words{a}", align_bytes=64) for a in range(2)]
+        plane = keep.tile([P, T], U8, name="plane", align_bytes=64)
+        gwords = [keep.tile([P, E * C], U32, name=f"gwords{a}", align_bytes=64) for a in range(2)]
+        gplane = keep.tile([P, E * C], U8, name="gplane", align_bytes=64)
+        w8 = keep.tile([P, E, 4 * N], U8, name="w8", align_bytes=64)
+        w4 = keep.tile([P, E, 2 * N], U8, name="w4", align_bytes=64)
+        ws = keep.tile([P, 2, E, N], U8, name="ws", align_bytes=64)
+        b_t = keep.tile([P, E], F32, name="b_t")
+        gate_t = keep.tile([P, E * C], F32, name="gate_t")
+        y = [keep.tile([P, C], F32, name=f"y{e}") for e in range(E)]
+        out_t = keep.tile([P, T], F32, name="out_t")
+        warm = keep.tile([P, 1], F32, name="warm")
+        acc = [[psum.tile([P, 512], F32, name=f"acc{e}{h}") for h in range(2)] for e in range(E)]
+
+        xv = [xT[512 * a : 512 * (a + 1), :].rearrange("(p j) t -> p j t", j=4) for a in range(2)]
+        for a in range(2):
+            for i, (s, e) in enumerate(CHUNKS[a]):
+                nc.sync.dma_start(out=x_t[a][i][:], in_=xv[a][:, :, s:e])
+            if a == 0:
+                nc.sync.dma_start(out=offs_t[:], in_=offs)
+        nc.vector.memset(ws[:].rearrange("p f e n -> p (f e n)").bitcast(I32), 0)
+        nc.vector.memset(warm[:], 0.0)
+        nc.vector.memset(plane[:].bitcast(I32), 0)
+        nc.vector.memset(out_t[:], 0.0)
+        for f, (src, queue) in enumerate(((w8_scales, nc.scalar), (w4_scales, nc.gpsimd))):
+            for q in range(4):
+                queue.dma_start(
+                    out=ws[32 * q : 32 * q + 4, f, :, :].bitcast(I32),
+                    in_=src[:, 0, 4 * q : 4 * q + 4, :].rearrange("e q n -> q e n").bitcast(I32),
+                )
+        nc.gpsimd.dma_start(out=b_t[:], in_=b)
+        nc.scalar.activation(warm[:], warm[:], ACT.Gelu_apprx_tanh)
+        nc.sync.dma_start(out=w8[:].bitcast(I32), in_=w8_words.rearrange("e a p n r -> p (e a) (n r)").bitcast(I32))
+        nc.sync.dma_start(out=w4[:].bitcast(I32), in_=w4_words.rearrange("e a p n -> p (e a) n").bitcast(I32))
+        nc.sync.dma_start(out=gate_t[:], in_=gate)
+        nc.sync.dma_start(out=dst_t[:], in_=dst)
+
+        def cast(engine, a, s, e):
+            i = 0 if e <= CHUNKS[a][0][1] else 1
+            c0 = CHUNKS[a][i][0]
+            copy = nc.scalar.copy if engine == "S" else nc.vector.tensor_copy
+            copy(
+                xb[a][:, s:e, :].rearrange("p (c i) j -> p c j i", i=4),
+                x_t[a][i][:, :, s - c0 : e - c0].rearrange("p j (c i) -> p c j i", i=4),
+            )
+
+        def quant(a, s, e):
+            nc.vector.quantize_mx(
+                out=words[a][:, s:e].bitcast(FP8X4),
+                scales=plane[PLANE[a] :, s:e],
+                in_=xb[a][:, s:e, :].rearrange("p t j -> p (t j)"),
+            )
+
+        def lists(t, e):
+            return t[:, 16 * e : 16 * (e + 1)]
+
+        def gather(out_tile, table, e):
+            nc.vector.tensor_copy(out_tile[:, C * e : C * (e + 1)], table[:].indirect(lists(offs_t, e)))
+
+        cast("S", 0, 0, 192)
+        cast("V", 0, 192, 384)
+        quant(0, 0, 256)
+        quant(0, 256, 384)
+        cast("S", 0, 544, 640)
+        cast("V", 0, 384, 544)
+        quant(0, 384, 640)
+        cast("S", 1, 0, 256)
+        for e in range(E):
+            gather(gwords[0], words[0], e)
+        cast("V", 1, 256, 384)
+        cast("S", 1, 544, 640)
+        cast("V", 1, 384, 544)
+        quant(1, 0, 256)
+        quant(1, 256, 384)
+        quant(1, 384, 640)
+        for e in range(E):
+            gather(gplane, plane, e)
+            gather(gwords[1], words[1], e)
+            halves = [slice(C * e + 128 * h, C * e + 128 * (h + 1)) for h in range(2)]
+            for a, w in enumerate((w8[:, e, :].bitcast(FP8X4), w4[:, e, :].bitcast(FP4X4))):
+                for h, cols in enumerate(halves):
+                    nc.tensor.matmul_mx(
+                        out=acc[e][h][:, :128], lhsT=w, lhsT_scale=ws[:, a, e, :],
+                        rhs=gwords[a][:, cols].bitcast(FP8X4), rhs_scale=gplane[PLANE[a] :, cols], start=(a == 0), stop=(a == 1),
+                    )
+            for h in range(2):
+                nc.scalar.activation(y[e][:, 128 * h : 128 * (h + 1)], acc[e][h][:, :128], ACT.Gelu_apprx_tanh, bias=b_t[:, e : e + 1])
+        for e in range(E):
+            nc.vector.tensor_tensor(out_t[:].indirect(lists(dst_t, e)), y[e][:], gate_t[:, C * e : C * (e + 1)], MULT)
+        nc.sync.dma_start(out=out, in_=out_t[:])

@@ -15,10 +15,6 @@ ACT = mybir.ActivationFunctionType
 MULT = mybir.AluOpType.mult
 
 P = 128
-CHUNKS = {
-    0: [(0, 384), (384, 640)],
-    1: [(0, 384), (384, 640)],
-}
 PLANE = [4, 0]
 
 
@@ -32,7 +28,7 @@ def tile_moe_two_lin_gelu_kernel(
     ):
         offs_t = keep.tile([P, E * C // 16], U16, name="offs_t")
         dst_t = keep.tile([P, E * C // 16], U16, name="dst_t")
-        x_t = [[keep.tile([P, 4, e - s], F32, name=f"x{a}{i}", align_bytes=64) for i, (s, e) in enumerate(CHUNKS[a])] for a in range(2)]
+        x_t = [[keep.tile([P, 2, T], F32, name=f"x{a}{h}", align_bytes=64) for h in range(2)] for a in range(2)]
         xb = [keep.tile([P, T, 4], BF16, name=f"xb{a}", align_bytes=64) for a in range(2)]
         words = [keep.tile([P, T], U32, name=f"words{a}", align_bytes=64) for a in range(2)]
         plane = keep.tile([P, T], U8, name="plane", align_bytes=64)
@@ -50,8 +46,8 @@ def tile_moe_two_lin_gelu_kernel(
 
         xv = [xT[512 * a : 512 * (a + 1), :].rearrange("(p j) t -> p j t", j=4) for a in range(2)]
         for a in range(2):
-            for i, (s, e) in enumerate(CHUNKS[a]):
-                nc.sync.dma_start(out=x_t[a][i][:], in_=xv[a][:, :, s:e])
+            for h in range(2):
+                nc.sync.dma_start(out=x_t[a][h][:], in_=xv[a][:, 2 * h : 2 * h + 2, :])
             if a == 0:
                 nc.sync.dma_start(out=offs_t[:], in_=offs)
         nc.vector.memset(ws[:].rearrange("p f e n -> p (f e n)").bitcast(I32), 0)
@@ -71,13 +67,11 @@ def tile_moe_two_lin_gelu_kernel(
         nc.sync.dma_start(out=gate_t[:], in_=gate)
         nc.sync.dma_start(out=dst_t[:], in_=dst)
 
-        def cast(engine, a, s, e):
-            i = 0 if e <= CHUNKS[a][0][1] else 1
-            c0 = CHUNKS[a][i][0]
+        def cast(engine, a, h, s, e):
             copy = nc.scalar.copy if engine == "S" else nc.vector.tensor_copy
             copy(
-                xb[a][:, s:e, :].rearrange("p (c i) j -> p c j i", i=4),
-                x_t[a][i][:, :, s - c0 : e - c0].rearrange("p j (c i) -> p c j i", i=4),
+                xb[a][:, s:e, 2 * h : 2 * h + 2].rearrange("p (c i) j -> p c j i", i=4),
+                x_t[a][h][:, :, s:e].rearrange("p j (c i) -> p c j i", i=4),
             )
 
         def quant(a, s, e):
@@ -93,22 +87,24 @@ def tile_moe_two_lin_gelu_kernel(
         def gather(out_tile, table, e):
             nc.vector.tensor_copy(out_tile[:, C * e : C * (e + 1)], table[:].indirect(lists(offs_t, e)))
 
-        cast("S", 0, 0, 192)
-        cast("V", 0, 192, 384)
+        cast("S", 0, 0, 432, 640)
+        cast("V", 0, 0, 0, 432)
+        cast("S", 0, 1, 384, 640)
+        cast("V", 0, 1, 0, 256)
+        cast("V", 0, 1, 256, 384)
         quant(0, 0, 256)
         quant(0, 256, 384)
-        cast("S", 0, 544, 640)
-        cast("V", 0, 384, 544)
         quant(0, 384, 640)
-        cast("S", 1, 0, 256)
+        cast("S", 1, 0, 0, 448)
+        cast("V", 1, 0, 448, 640)
         for e in range(E):
             gather(gwords[0], words[0], e)
-        cast("V", 1, 256, 384)
-        cast("S", 1, 544, 640)
-        cast("V", 1, 384, 544)
+        cast("S", 1, 1, 256, 512)
+        cast("S", 1, 1, 512, 640)
+        cast("V", 1, 1, 0, 256)
         quant(1, 0, 256)
-        quant(1, 256, 384)
-        quant(1, 384, 640)
+        quant(1, 256, 512)
+        quant(1, 512, 640)
         for e in range(E):
             gather(gplane, plane, e)
             gather(gwords[1], words[1], e)

@@ -15,6 +15,8 @@ ACT = mybir.ActivationFunctionType
 MULT = mybir.AluOpType.mult
 
 P = 128
+W = 640
+LOADS = [(0, 0, 2, 0, 640), (0, 2, 4, 0, 640), (1, 0, 4, 0, 384), (1, 0, 4, 384, 640)]
 PLANE = [4, 0]
 
 
@@ -28,10 +30,10 @@ def tile_moe_two_lin_gelu_kernel(
     ):
         offs_t = keep.tile([P, E * C // 16], U16, name="offs_t")
         dst_t = keep.tile([P, E * C // 16], U16, name="dst_t")
-        x_t = [[keep.tile([P, 2, T], F32, name=f"x{a}{h}", align_bytes=64) for h in range(2)] for a in range(2)]
+        x_t = [keep.tile([P, j1 - j0, e - s], F32, name=f"x{i}", align_bytes=64) for i, (a, j0, j1, s, e) in enumerate(LOADS)]
         xb = [keep.tile([P, T, 4], BF16, name=f"xb{a}", align_bytes=64) for a in range(2)]
-        words = [keep.tile([P, T], U32, name=f"words{a}", align_bytes=64) for a in range(2)]
-        plane = keep.tile([P, T], U8, name="plane", align_bytes=64)
+        words = [keep.tile([P, W], U32, name=f"words{a}", align_bytes=64) for a in range(2)]
+        plane = keep.tile([P, W], U8, name="plane", align_bytes=64)
         gwords = [keep.tile([P, E * C], U32, name=f"gwords{a}", align_bytes=64) for a in range(2)]
         gplane = keep.tile([P, E * C], U8, name="gplane", align_bytes=64)
         w8 = keep.tile([P, E, 4 * N], U8, name="w8", align_bytes=64)
@@ -45,33 +47,30 @@ def tile_moe_two_lin_gelu_kernel(
         acc = [[psum.tile([P, 512], F32, name=f"acc{e}{h}") for h in range(2)] for e in range(E)]
 
         xv = [xT[512 * a : 512 * (a + 1), :].rearrange("(p j) t -> p j t", j=4) for a in range(2)]
-        for a in range(2):
-            for h in range(2):
-                nc.sync.dma_start(out=x_t[a][h][:], in_=xv[a][:, 2 * h : 2 * h + 2, :])
-            if a == 0:
-                nc.sync.dma_start(out=offs_t[:], in_=offs)
-        nc.vector.memset(ws[:].rearrange("p f e n -> p (f e n)").bitcast(I32), 0)
-        nc.vector.memset(warm[:], 0.0)
-        nc.vector.memset(plane[:].bitcast(I32), 0)
-        nc.vector.memset(out_t[:], 0.0)
-        for f, (src, queue) in enumerate(((w8_scales, nc.scalar), (w4_scales, nc.gpsimd))):
-            for q in range(4):
+
+        def load_x(i):
+            a, j0, j1, s, e = LOADS[i]
+            nc.sync.dma_start(out=x_t[i][:], in_=xv[a][:, j0:j1, s:e])
+
+        def load_scales(f, src, queue, quadrants=range(4)):
+            for q in quadrants:
                 queue.dma_start(
                     out=ws[32 * q : 32 * q + 4, f, :, :].bitcast(I32),
                     in_=src[:, 0, 4 * q : 4 * q + 4, :].rearrange("e q n -> q e n").bitcast(I32),
                 )
-        nc.gpsimd.dma_start(out=b_t[:], in_=b)
-        nc.scalar.activation(warm[:], warm[:], ACT.Gelu_apprx_tanh)
-        nc.sync.dma_start(out=w8[:].bitcast(I32), in_=w8_words.rearrange("e a p n r -> p (e a) (n r)").bitcast(I32))
-        nc.sync.dma_start(out=w4[:].bitcast(I32), in_=w4_words.rearrange("e a p n -> p (e a) n").bitcast(I32))
-        nc.sync.dma_start(out=gate_t[:], in_=gate)
-        nc.sync.dma_start(out=dst_t[:], in_=dst)
 
-        def cast(engine, a, h, s, e):
+        def load_w8():
+            nc.sync.dma_start(out=w8[:].bitcast(I32), in_=w8_words.rearrange("e a p n r -> p (e a) (n r)").bitcast(I32))
+
+        def load_w4():
+            nc.sync.dma_start(out=w4[:].bitcast(I32), in_=w4_words.rearrange("e a p n -> p (e a) n").bitcast(I32))
+
+        def cast(engine, i, s, e):
+            a, j0, j1, c0, c1 = LOADS[i]
             copy = nc.scalar.copy if engine == "S" else nc.vector.tensor_copy
             copy(
-                xb[a][:, s:e, 2 * h : 2 * h + 2].rearrange("p (c i) j -> p c j i", i=4),
-                x_t[a][h][:, :, s:e].rearrange("p j (c i) -> p c j i", i=4),
+                xb[a][:, s:e, j0:j1].rearrange("p (c i) j -> p c j i", i=4),
+                x_t[i][:, :, s - c0 : e - c0].rearrange("p j (c i) -> p c j i", i=4),
             )
 
         def quant(a, s, e):
@@ -81,33 +80,10 @@ def tile_moe_two_lin_gelu_kernel(
                 in_=xb[a][:, s:e, :].rearrange("p t j -> p (t j)"),
             )
 
-        def lists(t, e):
-            return t[:, 16 * e : 16 * (e + 1)]
+        def gather(out_tile, table, s, e):
+            nc.vector.tensor_copy(out_tile[:, s:e], table[:].indirect(offs_t[:, s // 16 : e // 16]))
 
-        def gather(out_tile, table, e):
-            nc.vector.tensor_copy(out_tile[:, C * e : C * (e + 1)], table[:].indirect(lists(offs_t, e)))
-
-        cast("S", 0, 0, 432, 640)
-        cast("V", 0, 0, 0, 432)
-        cast("S", 0, 1, 384, 640)
-        cast("V", 0, 1, 0, 256)
-        cast("V", 0, 1, 256, 384)
-        quant(0, 0, 256)
-        quant(0, 256, 384)
-        quant(0, 384, 640)
-        cast("S", 1, 0, 0, 448)
-        cast("V", 1, 0, 448, 640)
-        for e in range(E):
-            gather(gwords[0], words[0], e)
-        cast("S", 1, 1, 256, 512)
-        cast("S", 1, 1, 512, 640)
-        cast("V", 1, 1, 0, 256)
-        quant(1, 0, 256)
-        quant(1, 256, 512)
-        quant(1, 512, 640)
-        for e in range(E):
-            gather(gplane, plane, e)
-            gather(gwords[1], words[1], e)
+        def experts(e):
             halves = [slice(C * e + 128 * h, C * e + 128 * (h + 1)) for h in range(2)]
             for a, w in enumerate((w8[:, e, :].bitcast(FP8X4), w4[:, e, :].bitcast(FP4X4))):
                 for h, cols in enumerate(halves):
@@ -117,6 +93,48 @@ def tile_moe_two_lin_gelu_kernel(
                     )
             for h in range(2):
                 nc.scalar.activation(y[e][:, 128 * h : 128 * (h + 1)], acc[e][h][:, :128], ACT.Gelu_apprx_tanh, bias=b_t[:, e : e + 1])
+
+        def scatter(e):
+            nc.vector.tensor_tensor(out_t[:].indirect(dst_t[:, 16 * e : 16 * (e + 1)]), y[e][:], gate_t[:, C * e : C * (e + 1)], MULT)
+
+        load_x(0)
+        load_x(1)
+        nc.sync.dma_start(out=offs_t[:], in_=offs)
+        load_x(2)
+        load_x(3)
+        nc.vector.memset(ws[:].rearrange("p f e n -> p (f e n)").bitcast(I32), 0)
+        nc.vector.memset(warm[:], 0.0)
+        nc.vector.memset(plane[:].bitcast(I32), 0)
+        nc.vector.memset(out_t[:], 0.0)
+        load_scales(0, w8_scales, nc.scalar)
+        load_scales(1, w4_scales, nc.gpsimd)
+        nc.gpsimd.dma_start(out=b_t[:], in_=b)
+        nc.scalar.activation(warm[:], warm[:], ACT.Gelu_apprx_tanh)
+        load_w8()
+        load_w4()
+        nc.sync.dma_start(out=gate_t[:], in_=gate)
+        nc.sync.dma_start(out=dst_t[:], in_=dst)
+        cast("S", 0, 432, 640)
+        cast("V", 0, 0, 432)
+        cast("S", 1, 384, 640)
+        cast("V", 1, 0, 256)
+        cast("V", 1, 256, 384)
+        quant(0, 0, 256)
+        quant(0, 256, 384)
+        quant(0, 384, 640)
+        cast("S", 2, 0, 256)
+        gather(gwords[0], words[0], 0, 256)
+        gather(gwords[0], words[0], 256, 512)
+        cast("V", 2, 256, 384)
+        cast("S", 3, 576, 640)
+        cast("V", 3, 384, 576)
+        quant(1, 0, 256)
+        quant(1, 256, 384)
+        quant(1, 384, 640)
         for e in range(E):
-            nc.vector.tensor_tensor(out_t[:].indirect(lists(dst_t, e)), y[e][:], gate_t[:, C * e : C * (e + 1)], MULT)
+            gather(gplane, plane, C * e, C * (e + 1))
+            gather(gwords[1], words[1], C * e, C * (e + 1))
+            experts(e)
+        for e in range(E):
+            scatter(e)
         nc.sync.dma_start(out=out, in_=out_t[:])

@@ -15,7 +15,7 @@ ACT = mybir.ActivationFunctionType
 MULT = mybir.AluOpType.mult
 
 P = 128
-W = 640
+W = 704
 LOADS = [(0, 0, 2, 0, 640), (0, 2, 4, 0, 640), (1, 0, 4, 0, 384), (1, 0, 4, 384, 640)]
 PLANE = [4, 0]
 
@@ -81,7 +81,7 @@ def tile_moe_two_lin_gelu_kernel(
             )
 
         def gather(out_tile, table, s, e):
-            nc.vector.tensor_copy(out_tile[:, s:e], table[:].indirect(offs_t[:, s // 16 : e // 16]))
+            nc.vector.tensor_copy(out_tile[:, s:e], table[:, : (W if e - s == E * C else T)].indirect(offs_t[:, s // 16 : e // 16]))
 
         def experts(e):
             halves = [slice(C * e + 128 * h, C * e + 128 * (h + 1)) for h in range(2)]
@@ -104,6 +104,7 @@ def tile_moe_two_lin_gelu_kernel(
         load_x(3)
         nc.vector.memset(ws[:].rearrange("p f e n -> p (f e n)").bitcast(I32), 0)
         nc.vector.memset(warm[:], 0.0)
+        nc.vector.memset(words[0][:, T:].bitcast(I32), 0)
         nc.vector.memset(plane[:].bitcast(I32), 0)
         nc.vector.memset(out_t[:], 0.0)
         load_scales(0, w8_scales, nc.scalar)
@@ -123,18 +124,20 @@ def tile_moe_two_lin_gelu_kernel(
         quant(0, 256, 384)
         quant(0, 384, 640)
         cast("S", 2, 0, 256)
-        gather(gwords[0], words[0], 0, 256)
-        gather(gwords[0], words[0], 256, 512)
+        gather(gwords[0], words[0], 0, 512)
         cast("V", 2, 256, 384)
-        cast("S", 3, 576, 640)
-        cast("V", 3, 384, 576)
+        cast("V", 3, 384, 512)
+        cast("S", 3, 512, 640)
         quant(1, 0, 256)
-        quant(1, 256, 384)
-        quant(1, 384, 640)
-        for e in range(E):
-            gather(gplane, plane, C * e, C * (e + 1))
-            gather(gwords[1], words[1], C * e, C * (e + 1))
-            experts(e)
+        quant(1, 256, 512)
+        quant(1, 512, 640)
+        gather(gplane, plane, 0, 256)
+        gather(gwords[1], words[1], 0, 128)
+        gather(gwords[1], words[1], 128, 256)
+        experts(0)
+        gather(gplane, plane, 256, 512)
+        gather(gwords[1], words[1], 256, 512)
+        experts(1)
         for e in range(E):
             scatter(e)
         nc.sync.dma_start(out=out, in_=out_t[:])

@@ -16,7 +16,7 @@ MULT = mybir.AluOpType.mult
 
 P = 128
 W = 704
-LOADS = [(0, 0, 2, 0, 640), (0, 2, 4, 0, 640), (1, 0, 4, 0, 384), (1, 0, 4, 384, 640)]
+LOADS = [(0, 0, 2, 0, 640), (0, 2, 4, 0, 640), (1, 0, 4, 0, 256), (1, 0, 4, 256, 512), (1, 0, 4, 512, 640)]
 PLANE = [4, 0]
 
 
@@ -31,7 +31,7 @@ def tile_moe_two_lin_gelu_kernel(
         offs_t = keep.tile([P, E * C // 16], U16, name="offs_t")
         dst_t = keep.tile([P, E * C // 16], U16, name="dst_t")
         x_t = [keep.tile([P, j1 - j0, e - s], F32, name=f"x{i}", align_bytes=64) for i, (a, j0, j1, s, e) in enumerate(LOADS)]
-        xb = [keep.tile([P, T, 4], BF16, name=f"xb{a}", align_bytes=64) for a in range(2)]
+        xb = [keep.tile([P, T, 4], BF16, name=f"xb{a}", tag=f"xb{a}", align_bytes=64) for a in range(2)]
         words = [keep.tile([P, W], U32, name=f"words{a}", align_bytes=64) for a in range(2)]
         plane = keep.tile([P, W], U8, name="plane", align_bytes=64)
         gwords = [keep.tile([P, E * C], U32, name=f"gwords{a}", align_bytes=64) for a in range(2)]
@@ -44,7 +44,6 @@ def tile_moe_two_lin_gelu_kernel(
         y = [keep.tile([P, C], F32, name=f"y{e}") for e in range(E)]
         out_t = keep.tile([P, T], F32, name="out_t")
         warm = keep.tile([P, 1], F32, name="warm")
-        acc = [[psum.tile([P, 512], F32, name=f"acc{e}{h}") for h in range(2)] for e in range(E)]
 
         xv = [xT[512 * a : 512 * (a + 1), :].rearrange("(p j) t -> p j t", j=4) for a in range(2)]
 
@@ -84,15 +83,16 @@ def tile_moe_two_lin_gelu_kernel(
             nc.vector.tensor_copy(out_tile[:, s:e], table[:, : (W if e - s == E * C else T)].indirect(offs_t[:, s // 16 : e // 16]))
 
         def experts(e):
+            acc = [psum.tile([P, 512], F32, name=f"acc{e}{h}", tag=f"acc{h}") for h in range(2)]
             halves = [slice(C * e + 128 * h, C * e + 128 * (h + 1)) for h in range(2)]
             for a, w in enumerate((w8[:, e, :].bitcast(FP8X4), w4[:, e, :].bitcast(FP4X4))):
                 for h, cols in enumerate(halves):
                     nc.tensor.matmul_mx(
-                        out=acc[e][h][:, :128], lhsT=w, lhsT_scale=ws[:, a, e, :],
+                        out=acc[h][:, :128], lhsT=w, lhsT_scale=ws[:, a, e, :],
                         rhs=gwords[a][:, cols].bitcast(FP8X4), rhs_scale=gplane[PLANE[a] :, cols], start=(a == 0), stop=(a == 1),
                     )
             for h in range(2):
-                nc.scalar.activation(y[e][:, 128 * h : 128 * (h + 1)], acc[e][h][:, :128], ACT.Gelu_apprx_tanh, bias=b_t[:, e : e + 1])
+                nc.scalar.activation(y[e][:, 128 * h : 128 * (h + 1)], acc[h][:, :128], ACT.Gelu_apprx_tanh, bias=b_t[:, e : e + 1])
 
         def scatter(e):
             nc.vector.tensor_tensor(out_t[:].indirect(dst_t[:, 16 * e : 16 * (e + 1)]), y[e][:], gate_t[:, C * e : C * (e + 1)], MULT)
@@ -102,17 +102,19 @@ def tile_moe_two_lin_gelu_kernel(
         nc.sync.dma_start(out=offs_t[:], in_=offs)
         load_x(2)
         load_x(3)
+        load_x(4)
         nc.vector.memset(ws[:].rearrange("p f e n -> p (f e n)").bitcast(I32), 0)
         nc.vector.memset(warm[:], 0.0)
         nc.vector.memset(words[0][:, T:].bitcast(I32), 0)
         nc.vector.memset(plane[:].bitcast(I32), 0)
         nc.vector.memset(out_t[:], 0.0)
-        load_scales(0, w8_scales, nc.scalar)
+        load_scales(0, w8_scales, nc.scalar, range(2))
         load_scales(1, w4_scales, nc.gpsimd)
-        nc.gpsimd.dma_start(out=b_t[:], in_=b)
         nc.scalar.activation(warm[:], warm[:], ACT.Gelu_apprx_tanh)
         load_w8()
         load_w4()
+        load_scales(0, w8_scales, nc.sync, range(2, 4))
+        nc.sync.dma_start(out=b_t[:], in_=b)
         nc.sync.dma_start(out=gate_t[:], in_=gate)
         nc.sync.dma_start(out=dst_t[:], in_=dst)
         cast("S", 0, 432, 640)
@@ -125,10 +127,10 @@ def tile_moe_two_lin_gelu_kernel(
         quant(0, 384, 640)
         cast("S", 2, 0, 256)
         gather(gwords[0], words[0], 0, 512)
-        cast("V", 2, 256, 384)
-        cast("V", 3, 384, 512)
-        cast("S", 3, 512, 640)
+        cast("S", 3, 256, 448)
         quant(1, 0, 256)
+        cast("V", 3, 448, 512)
+        cast("V", 4, 512, 640)
         quant(1, 256, 512)
         quant(1, 512, 640)
         gather(gplane, plane, 0, 256)

@@ -16,7 +16,7 @@ MULT = mybir.AluOpType.mult
 
 P = 128
 W = 704
-LOADS = [(0, 0, 2, 0, 640), (0, 2, 4, 0, 640), (1, 0, 4, 0, 256), (1, 0, 4, 256, 512), (1, 0, 4, 512, 640)]
+LOADS = [(0, 0, 2, 0, 640), (0, 2, 4, 0, 640)]
 PLANE = [4, 0]
 
 
@@ -31,6 +31,8 @@ def tile_moe_two_lin_gelu_kernel(
         offs_t = keep.tile([P, E * C // 16], U16, name="offs_t")
         dst_t = keep.tile([P, E * C // 16], U16, name="dst_t")
         x_t = [keep.tile([P, j1 - j0, e - s], F32, name=f"x{i}", align_bytes=64) for i, (a, j0, j1, s, e) in enumerate(LOADS)]
+        x1 = keep.tile([P, 4 * T], F32, name="x1flat", align_bytes=64)
+        x1_rows = x1[:].rearrange("p (j t) -> p j t", j=4)
         xb = [keep.tile([P, T, 4], BF16, name=f"xb{a}", tag=f"xb{a}", align_bytes=64) for a in range(2)]
         words = [keep.tile([P, W], U32, name=f"words{a}", align_bytes=64) for a in range(2)]
         plane = keep.tile([P, W], U8, name="plane", align_bytes=64)
@@ -50,6 +52,24 @@ def tile_moe_two_lin_gelu_kernel(
         def load_x(i):
             a, j0, j1, s, e = LOADS[i]
             nc.sync.dma_start(out=x_t[i][:], in_=xv[a][:, j0:j1, s:e])
+
+        def load_x1(i):
+            src = xT[512:, :].rearrange("(p j) t -> p (j t)", j=4)
+            if i < 2:
+                cols = slice(2 * T * i, 2 * T * i + T + 384)
+                nc.sync.dma_start(out=x1[:, cols], in_=src[:, cols])
+            else:
+                nc.sync.dma_start(
+                    out=x1[:].rearrange("p (h c) -> p h c", h=2)[:, :, T + 384 :],
+                    in_=src.rearrange("p (h c) -> p h c", h=2)[:, :, T + 384 :],
+                )
+
+        def cast1(engine, j0, j1, s, e):
+            copy = nc.scalar.copy if engine == "S" else nc.vector.tensor_copy
+            copy(
+                xb[1][:, s:e, j0:j1].rearrange("p (c i) j -> p c j i", i=4),
+                x1_rows[:, j0:j1, s:e].rearrange("p j (c i) -> p c j i", i=4),
+            )
 
         def load_scales(f, src, queue, quadrants=range(4)):
             for q in quadrants:
@@ -100,9 +120,9 @@ def tile_moe_two_lin_gelu_kernel(
         load_x(0)
         load_x(1)
         nc.sync.dma_start(out=offs_t[:], in_=offs)
-        load_x(2)
-        load_x(3)
-        load_x(4)
+        load_x1(0)
+        load_x1(1)
+        load_x1(2)
         nc.vector.memset(ws[:].rearrange("p f e n -> p (f e n)").bitcast(I32), 0)
         nc.vector.memset(warm[:], 0.0)
         nc.vector.memset(words[0][:, T:].bitcast(I32), 0)
@@ -125,12 +145,14 @@ def tile_moe_two_lin_gelu_kernel(
         quant(0, 0, 256)
         quant(0, 256, 384)
         quant(0, 384, 640)
-        cast("S", 2, 0, 256)
+        cast1("V", 0, 2, 0, 128)
+        cast1("S", 0, 2, 128, 384)
         gather(gwords[0], words[0], 0, 512)
-        cast("S", 3, 256, 448)
+        cast1("S", 2, 4, 192, 384)
+        cast1("V", 2, 4, 0, 192)
+        cast1("V", 0, 4, 384, 512)
+        cast1("S", 0, 4, 512, 640)
         quant(1, 0, 256)
-        cast("V", 3, 448, 512)
-        cast("V", 4, 512, 640)
         quant(1, 256, 512)
         quant(1, 512, 640)
         gather(gplane, plane, 0, 256)

@@ -16,7 +16,7 @@ MULT = mybir.AluOpType.mult
 
 P = 128
 W = 704
-LOADS = [(0, 0, 2, 0, 640), (0, 2, 4, 0, 640)]
+LOADS = [(0, 0, 1024, 1, 0), (0, 1280, 1024, 1, 0), (0, 1024, 256, 2, 1280), (1, 0, 1024, 1, 0), (1, 1280, 1024, 1, 0), (1, 1024, 256, 2, 1280)]
 PLANE = [4, 0]
 
 
@@ -30,9 +30,7 @@ def tile_moe_two_lin_gelu_kernel(
     ):
         offs_t = keep.tile([P, E * C // 16], U16, name="offs_t")
         dst_t = keep.tile([P, E * C // 16], U16, name="dst_t")
-        x_t = [keep.tile([P, j1 - j0, e - s], F32, name=f"x{i}", align_bytes=64) for i, (a, j0, j1, s, e) in enumerate(LOADS)]
-        x1 = keep.tile([P, 4 * T], F32, name="x1flat", align_bytes=64)
-        x1_rows = x1[:].rearrange("p (j t) -> p j t", j=4)
+        x_t = [keep.tile([P, 4 * T], F32, name=f"x{a}", align_bytes=64) for a in range(2)]
         xb = [keep.tile([P, T, 4], BF16, name=f"xb{a}", tag=f"xb{a}", align_bytes=64) for a in range(2)]
         words = [keep.tile([P, W], U32, name=f"words{a}", align_bytes=64) for a in range(2)]
         plane = keep.tile([P, W], U8, name="plane", align_bytes=64)
@@ -47,29 +45,18 @@ def tile_moe_two_lin_gelu_kernel(
         out_t = keep.tile([P, T], F32, name="out_t")
         warm = keep.tile([P, 1], F32, name="warm")
 
-        xv = [xT[512 * a : 512 * (a + 1), :].rearrange("(p j) t -> p j t", j=4) for a in range(2)]
 
         def load_x(i):
-            a, j0, j1, s, e = LOADS[i]
-            nc.sync.dma_start(out=x_t[i][:], in_=xv[a][:, j0:j1, s:e])
-
-        def load_x1(i):
-            src = xT[512:, :].rearrange("(p j) t -> p (j t)", j=4)
-            if i < 2:
-                cols = slice(2 * T * i, 2 * T * i + T + 384)
-                nc.sync.dma_start(out=x1[:, cols], in_=src[:, cols])
+            a, first, length, pieces, distance = LOADS[i]
+            src = xT[512 * a : 512 * (a + 1), :].rearrange("(p j) t -> p (j t)", j=4)
+            if pieces == 1:
+                nc.sync.dma_start(out=x_t[a][:, first : first + length], in_=src[:, first : first + length])
             else:
+                g0, c0 = divmod(first, distance)
                 nc.sync.dma_start(
-                    out=x1[:].rearrange("p (h c) -> p h c", h=2)[:, :, T + 384 :],
-                    in_=src.rearrange("p (h c) -> p h c", h=2)[:, :, T + 384 :],
+                    out=x_t[a][:].rearrange("p (g c) -> p g c", c=distance)[:, g0 : g0 + pieces, c0 : c0 + length],
+                    in_=src.rearrange("p (g c) -> p g c", c=distance)[:, g0 : g0 + pieces, c0 : c0 + length],
                 )
-
-        def cast1(engine, j0, j1, s, e):
-            copy = nc.scalar.copy if engine == "S" else nc.vector.tensor_copy
-            copy(
-                xb[1][:, s:e, j0:j1].rearrange("p (c i) j -> p c j i", i=4),
-                x1_rows[:, j0:j1, s:e].rearrange("p j (c i) -> p c j i", i=4),
-            )
 
         def load_scales(f, src, queue, quadrants=range(4)):
             for q in quadrants:
@@ -84,12 +71,11 @@ def tile_moe_two_lin_gelu_kernel(
         def load_w4():
             nc.sync.dma_start(out=w4[:].bitcast(I32), in_=w4_words.rearrange("e a p n -> p (e a) n").bitcast(I32))
 
-        def cast(engine, i, s, e):
-            a, j0, j1, c0, c1 = LOADS[i]
+        def cast(engine, a, j0, j1, s, e):
             copy = nc.scalar.copy if engine == "S" else nc.vector.tensor_copy
             copy(
                 xb[a][:, s:e, j0:j1].rearrange("p (c i) j -> p c j i", i=4),
-                x_t[i][:, :, s - c0 : e - c0].rearrange("p j (c i) -> p c j i", i=4),
+                x_t[a][:].rearrange("p (j t) -> p j t", j=4)[:, j0:j1, s:e].rearrange("p j (c i) -> p c j i", i=4),
             )
 
         def quant(a, s, e):
@@ -119,39 +105,39 @@ def tile_moe_two_lin_gelu_kernel(
 
         load_x(0)
         load_x(1)
+        load_x(2)
         nc.sync.dma_start(out=offs_t[:], in_=offs)
-        load_x1(0)
-        load_x1(1)
-        load_x1(2)
+        load_x(3)
+        load_x(4)
+        load_x(5)
         nc.vector.memset(ws[:].rearrange("p f e n -> p (f e n)").bitcast(I32), 0)
         nc.vector.memset(warm[:], 0.0)
         nc.vector.memset(words[0][:, T:].bitcast(I32), 0)
         nc.vector.memset(plane[:].bitcast(I32), 0)
         nc.vector.memset(out_t[:], 0.0)
-        load_scales(0, w8_scales, nc.scalar, range(2))
+        nc.gpsimd.dma_start(out=b_t[:], in_=b)
         load_scales(1, w4_scales, nc.gpsimd)
         nc.scalar.activation(warm[:], warm[:], ACT.Gelu_apprx_tanh)
         load_w8()
         load_w4()
-        load_scales(0, w8_scales, nc.sync, range(2, 4))
-        nc.sync.dma_start(out=b_t[:], in_=b)
+        load_scales(0, w8_scales, nc.sync)
         nc.sync.dma_start(out=gate_t[:], in_=gate)
         nc.sync.dma_start(out=dst_t[:], in_=dst)
-        cast("S", 0, 432, 640)
-        cast("V", 0, 0, 432)
-        cast("S", 1, 384, 640)
-        cast("V", 1, 0, 256)
-        cast("V", 1, 256, 384)
+        cast("S", 0, 0, 2, 304, 384)
+        cast("V", 0, 0, 2, 128, 304)
+        cast("V", 0, 2, 4, 128, 384)
+        cast("S", 0, 0, 4, 0, 128)
+        cast("V", 0, 0, 4, 384, 512)
+        cast("S", 0, 0, 4, 512, 640)
         quant(0, 0, 256)
-        quant(0, 256, 384)
-        quant(0, 384, 640)
-        cast1("V", 0, 2, 0, 128)
-        cast1("S", 0, 2, 128, 384)
+        quant(0, 256, 512)
+        quant(0, 512, 640)
+        cast("S", 1, 0, 2, 128, 384)
         gather(gwords[0], words[0], 0, 512)
-        cast1("S", 2, 4, 192, 384)
-        cast1("V", 2, 4, 0, 192)
-        cast1("V", 0, 4, 384, 512)
-        cast1("S", 0, 4, 512, 640)
+        cast("S", 1, 0, 4, 0, 128)
+        cast("V", 1, 2, 4, 128, 384)
+        cast("V", 1, 0, 4, 384, 512)
+        cast("S", 1, 0, 4, 512, 640)
         quant(1, 0, 256)
         quant(1, 256, 512)
         quant(1, 512, 640)

@@ -124,9 +124,9 @@ def tile_moe_two_lin_gelu_kernel(
         nc.sync.dma_start(out=gate_t[:], in_=gate)
         nc.sync.dma_start(out=dst_t[:], in_=dst)
         cast("S", 0, 0, 2, 304, 384)
-        cast("V", 0, 0, 2, 128, 304)
-        cast("V", 0, 2, 4, 128, 384)
-        cast("S", 0, 0, 4, 0, 128)
+        cast("V", 0, 0, 2, 96, 304)
+        cast("V", 0, 2, 4, 96, 384)
+        cast("S", 0, 0, 4, 0, 96)
         cast("V", 0, 0, 4, 384, 512)
         cast("S", 0, 0, 4, 512, 640)
         quant(0, 0, 256)

@@ -72,7 +72,7 @@ def tile_moe_two_lin_gelu_kernel(
             nc.sync.dma_start(out=w4[:].bitcast(I32), in_=w4_words.rearrange("e a p n -> p (e a) n").bitcast(I32))
 
         def cast(engine, a, j0, j1, s, e):
-            copy = nc.scalar.copy if engine == "S" else nc.vector.tensor_copy
+            copy = {"S": nc.scalar.copy, "V": nc.vector.tensor_copy, "G": nc.gpsimd.tensor_copy}[engine]
             copy(
                 xb[a][:, s:e, j0:j1].rearrange("p (c i) j -> p c j i", i=4),
                 x_t[a][:].rearrange("p (j t) -> p j t", j=4)[:, j0:j1, s:e].rearrange("p j (c i) -> p c j i", i=4),
@@ -115,14 +115,18 @@ def tile_moe_two_lin_gelu_kernel(
         nc.vector.memset(words[0][:, T:].bitcast(I32), 0)
         nc.vector.memset(plane[:].bitcast(I32), 0)
         nc.vector.memset(out_t[:], 0.0)
-        nc.gpsimd.dma_start(out=b_t[:], in_=b)
-        load_scales(1, w4_scales, nc.gpsimd)
         nc.scalar.activation(warm[:], warm[:], ACT.Gelu_apprx_tanh)
-        load_w8()
-        load_w4()
+        nc.sync.dma_start(out=w8[:, 0, :].bitcast(I32), in_=w8_words[0, 0].rearrange("p n r -> p (n r)").bitcast(I32))
         load_scales(0, w8_scales, nc.sync)
-        nc.sync.dma_start(out=gate_t[:], in_=gate)
+        load_scales(1, w4_scales, nc.sync, range(2))
+        nc.sync.dma_start(out=w4[:, 0, :].bitcast(I32), in_=w4_words[0, 0].bitcast(I32))
+        load_scales(1, w4_scales, nc.sync, range(2, 4))
+        nc.sync.dma_start(out=b_t[:], in_=b)
         nc.sync.dma_start(out=dst_t[:], in_=dst)
+        nc.sync.dma_start(out=gate_t[:, :C], in_=gate[:, :C])
+        nc.sync.dma_start(out=w8[:, 1, :].bitcast(I32), in_=w8_words[1, 0].rearrange("p n r -> p (n r)").bitcast(I32))
+        nc.sync.dma_start(out=w4[:, 1, :].bitcast(I32), in_=w4_words[1, 0].bitcast(I32))
+        nc.sync.dma_start(out=gate_t[:, C:], in_=gate[:, C:])
         cast("S", 0, 0, 2, 304, 384)
         cast("V", 0, 0, 2, 96, 304)
         cast("V", 0, 2, 4, 96, 384)

@@ -11,13 +11,21 @@ U16 = mybir.dt.uint16
 U8 = mybir.dt.uint8
 FP8X4 = mybir.dt.float8_e4m3fn_x4
 FP4X4 = mybir.dt.float4_e2m1fn_x4
-ACT = mybir.ActivationFunctionType
+GELU = mybir.ActivationFunctionType.Gelu_apprx_tanh
 MULT = mybir.AluOpType.mult
 
 P = 128
-W = 704
-LOADS = [(0, 0, 1024, 1, 0), (0, 1280, 1024, 1, 0), (0, 1024, 256, 2, 1280), (1, 0, 1024, 1, 0), (1, 1280, 1024, 1, 0), (1, 1024, 256, 2, 1280)]
-PLANE = [4, 0]
+SLOTS = E * C
+HALF = 128
+LIST_ROWS = 16
+SCALE_ROW = (4, 0)
+WIDE = T + 64
+
+EARLY = 384
+SCALAR_EARLY = 128
+SCALAR_LATE = 512
+FIRST_SPLIT = 304
+QUANT_RANGES = ((0, 256), (256, SCALAR_LATE), (SCALAR_LATE, T))
 
 
 def tile_moe_two_lin_gelu_kernel(
@@ -28,130 +36,123 @@ def tile_moe_two_lin_gelu_kernel(
         tc.tile_pool(name="keep", bufs=1) as keep,
         tc.psum_pool(name="psum", bufs=1) as psum,
     ):
-        offs_t = keep.tile([P, E * C // 16], U16, name="offs_t")
-        dst_t = keep.tile([P, E * C // 16], U16, name="dst_t")
-        x_t = [keep.tile([P, 4 * T], F32, name=f"x{a}", align_bytes=64) for a in range(2)]
-        xb = [keep.tile([P, T, 4], BF16, name=f"xb{a}", tag=f"xb{a}", align_bytes=64) for a in range(2)]
-        words = [keep.tile([P, W], U32, name=f"words{a}", align_bytes=64) for a in range(2)]
-        plane = keep.tile([P, W], U8, name="plane", align_bytes=64)
-        gwords = [keep.tile([P, E * C], U32, name=f"gwords{a}", align_bytes=64) for a in range(2)]
-        gplane = keep.tile([P, E * C], U8, name="gplane", align_bytes=64)
+        offs_t = keep.tile([P, SLOTS // LIST_ROWS], U16, name="offs_t")
+        dst_t = keep.tile([P, SLOTS // LIST_ROWS], U16, name="dst_t")
+        x_f32 = [keep.tile([P, 4 * T], F32, name=f"x_f32_{a}", align_bytes=64) for a in range(2)]
+        x_bf16 = [keep.tile([P, T, 4], BF16, name=f"x_bf16_{a}", align_bytes=64) for a in range(2)]
+        words = [keep.tile([P, width], U32, name=f"words{a}", align_bytes=64) for a, width in enumerate((WIDE, T))]
+        scales = keep.tile([P, T], U8, name="scales", align_bytes=64)
+        slot_words = [keep.tile([P, SLOTS], U32, name=f"slot_words{a}", align_bytes=64) for a in range(2)]
+        slot_scales = keep.tile([P, SLOTS], U8, name="slot_scales", align_bytes=64)
         w8 = keep.tile([P, E, 4 * N], U8, name="w8", align_bytes=64)
         w4 = keep.tile([P, E, 2 * N], U8, name="w4", align_bytes=64)
-        ws = keep.tile([P, 2, E, N], U8, name="ws", align_bytes=64)
+        w_scales = keep.tile([P, 2, E, N], U8, name="w_scales", align_bytes=64)
         b_t = keep.tile([P, E], F32, name="b_t")
-        gate_t = keep.tile([P, E * C], F32, name="gate_t")
+        gate_t = keep.tile([P, SLOTS], F32, name="gate_t")
         y = [keep.tile([P, C], F32, name=f"y{e}") for e in range(E)]
         out_t = keep.tile([P, T], F32, name="out_t")
         warm = keep.tile([P, 1], F32, name="warm")
 
-
-        def load_x(i):
-            a, first, length, pieces, distance = LOADS[i]
+        def load_pass(a):
             src = xT[512 * a : 512 * (a + 1), :].rearrange("(p j) t -> p (j t)", j=4)
-            if pieces == 1:
-                nc.sync.dma_start(out=x_t[a][:, first : first + length], in_=src[:, first : first + length])
-            else:
-                g0, c0 = divmod(first, distance)
-                nc.sync.dma_start(
-                    out=x_t[a][:].rearrange("p (g c) -> p g c", c=distance)[:, g0 : g0 + pieces, c0 : c0 + length],
-                    in_=src.rearrange("p (g c) -> p g c", c=distance)[:, g0 : g0 + pieces, c0 : c0 + length],
-                )
+            for pair in range(2):
+                run = slice(2 * T * pair, 2 * T * pair + T + EARLY)
+                nc.sync.dma_start(out=x_f32[a][:, run], in_=src[:, run])
+            nc.sync.dma_start(
+                out=x_f32[a][:].rearrange("p (pair c) -> p pair c", pair=2)[:, :, T + EARLY :],
+                in_=src.rearrange("p (pair c) -> p pair c", pair=2)[:, :, T + EARLY :],
+            )
 
-        def load_scales(f, src, queue, quadrants=range(4)):
+        def load_w_scales(a, src, quadrants):
             for q in quadrants:
-                queue.dma_start(
-                    out=ws[32 * q : 32 * q + 4, f, :, :].bitcast(I32),
+                nc.sync.dma_start(
+                    out=w_scales[32 * q : 32 * q + 4, a, :, :].bitcast(I32),
                     in_=src[:, 0, 4 * q : 4 * q + 4, :].rearrange("e q n -> q e n").bitcast(I32),
                 )
 
-        def load_w8():
-            nc.sync.dma_start(out=w8[:].bitcast(I32), in_=w8_words.rearrange("e a p n r -> p (e a) (n r)").bitcast(I32))
+        def load_w8(e):
+            nc.sync.dma_start(out=w8[:, e, :].bitcast(I32), in_=w8_words[e, 0].rearrange("p n r -> p (n r)").bitcast(I32))
 
-        def load_w4():
-            nc.sync.dma_start(out=w4[:].bitcast(I32), in_=w4_words.rearrange("e a p n -> p (e a) n").bitcast(I32))
+        def load_w4(e):
+            nc.sync.dma_start(out=w4[:, e, :].bitcast(I32), in_=w4_words[e, 0].bitcast(I32))
 
-        def cast(engine, a, j0, j1, s, e):
-            copy = {"S": nc.scalar.copy, "V": nc.vector.tensor_copy, "G": nc.gpsimd.tensor_copy}[engine]
+        def load_gate(e):
+            nc.sync.dma_start(out=gate_t[:, C * e : C * (e + 1)], in_=gate[:, C * e : C * (e + 1)])
+
+        def cast(copy, a, j0, j1, s, e):
             copy(
-                xb[a][:, s:e, j0:j1].rearrange("p (c i) j -> p c j i", i=4),
-                x_t[a][:].rearrange("p (j t) -> p j t", j=4)[:, j0:j1, s:e].rearrange("p j (c i) -> p c j i", i=4),
+                x_bf16[a][:, s:e, j0:j1].rearrange("p (c i) j -> p c j i", i=4),
+                x_f32[a][:].rearrange("p (j t) -> p j t", j=4)[:, j0:j1, s:e].rearrange("p j (c i) -> p c j i", i=4),
             )
 
-        def quant(a, s, e):
-            nc.vector.quantize_mx(
-                out=words[a][:, s:e].bitcast(FP8X4),
-                scales=plane[PLANE[a] :, s:e],
-                in_=xb[a][:, s:e, :].rearrange("p t j -> p (t j)"),
-            )
+        def finish_pass(a):
+            cast(nc.vector.tensor_copy, a, 2, 4, SCALAR_EARLY, EARLY)
+            cast(nc.scalar.copy, a, 0, 4, 0, SCALAR_EARLY)
+            cast(nc.vector.tensor_copy, a, 0, 4, EARLY, SCALAR_LATE)
+            cast(nc.scalar.copy, a, 0, 4, SCALAR_LATE, T)
+            for s, e in QUANT_RANGES:
+                nc.vector.quantize_mx(
+                    out=words[a][:, s:e].bitcast(FP8X4),
+                    scales=scales[SCALE_ROW[a] :, s:e],
+                    in_=x_bf16[a][:, s:e, :].rearrange("p t j -> p (t j)"),
+                )
 
-        def gather(out_tile, table, s, e):
-            nc.vector.tensor_copy(out_tile[:, s:e], table[:, : (W if e - s == E * C else T)].indirect(offs_t[:, s // 16 : e // 16]))
+        def gather(into, window, s, e):
+            nc.vector.tensor_copy(into[:, s:e], window.indirect(offs_t[:, s // LIST_ROWS : e // LIST_ROWS]))
 
-        def experts(e):
+        def expert(e):
             acc = [psum.tile([P, 512], F32, name=f"acc{e}{h}", tag=f"acc{h}") for h in range(2)]
-            halves = [slice(C * e + 128 * h, C * e + 128 * (h + 1)) for h in range(2)]
             for a, w in enumerate((w8[:, e, :].bitcast(FP8X4), w4[:, e, :].bitcast(FP4X4))):
-                for h, cols in enumerate(halves):
+                for h in range(2):
+                    cols = slice(C * e + HALF * h, C * e + HALF * (h + 1))
                     nc.tensor.matmul_mx(
-                        out=acc[h][:, :128], lhsT=w, lhsT_scale=ws[:, a, e, :],
-                        rhs=gwords[a][:, cols].bitcast(FP8X4), rhs_scale=gplane[PLANE[a] :, cols], start=(a == 0), stop=(a == 1),
+                        out=acc[h][:, :HALF],
+                        lhsT=w,
+                        lhsT_scale=w_scales[:, a, e, :],
+                        rhs=slot_words[a][:, cols].bitcast(FP8X4),
+                        rhs_scale=slot_scales[SCALE_ROW[a] :, cols],
+                        start=(a == 0),
+                        stop=(a == 1),
                     )
             for h in range(2):
-                nc.scalar.activation(y[e][:, 128 * h : 128 * (h + 1)], acc[h][:, :128], ACT.Gelu_apprx_tanh, bias=b_t[:, e : e + 1])
+                nc.scalar.activation(y[e][:, HALF * h : HALF * (h + 1)], acc[h][:, :HALF], GELU, bias=b_t[:, e : e + 1])
 
-        def scatter(e):
-            nc.vector.tensor_tensor(out_t[:].indirect(dst_t[:, 16 * e : 16 * (e + 1)]), y[e][:], gate_t[:, C * e : C * (e + 1)], MULT)
-
-        load_x(0)
-        load_x(1)
-        load_x(2)
+        load_pass(0)
         nc.sync.dma_start(out=offs_t[:], in_=offs)
-        load_x(3)
-        load_x(4)
-        load_x(5)
-        nc.vector.memset(ws[:].rearrange("p f e n -> p (f e n)").bitcast(I32), 0)
+        load_pass(1)
+        nc.vector.memset(w_scales[:].rearrange("p a e n -> p (a e n)").bitcast(I32), 0)
         nc.vector.memset(warm[:], 0.0)
         nc.vector.memset(words[0][:, T:].bitcast(I32), 0)
-        nc.vector.memset(plane[:].bitcast(I32), 0)
+        nc.vector.memset(scales[:].bitcast(I32), 0)
         nc.vector.memset(out_t[:], 0.0)
-        nc.scalar.activation(warm[:], warm[:], ACT.Gelu_apprx_tanh)
-        nc.sync.dma_start(out=w8[:, 0, :].bitcast(I32), in_=w8_words[0, 0].rearrange("p n r -> p (n r)").bitcast(I32))
-        load_scales(0, w8_scales, nc.sync)
-        load_scales(1, w4_scales, nc.sync, range(2))
-        nc.sync.dma_start(out=w4[:, 0, :].bitcast(I32), in_=w4_words[0, 0].bitcast(I32))
-        load_scales(1, w4_scales, nc.sync, range(2, 4))
+        nc.scalar.activation(warm[:], warm[:], GELU)
+        load_w8(0)
+        load_w_scales(0, w8_scales, range(4))
+        load_w_scales(1, w4_scales, range(2))
+        load_w4(0)
+        load_w_scales(1, w4_scales, range(2, 4))
         nc.sync.dma_start(out=b_t[:], in_=b)
         nc.sync.dma_start(out=dst_t[:], in_=dst)
-        nc.sync.dma_start(out=gate_t[:, :C], in_=gate[:, :C])
-        nc.sync.dma_start(out=w8[:, 1, :].bitcast(I32), in_=w8_words[1, 0].rearrange("p n r -> p (n r)").bitcast(I32))
-        nc.sync.dma_start(out=w4[:, 1, :].bitcast(I32), in_=w4_words[1, 0].bitcast(I32))
-        nc.sync.dma_start(out=gate_t[:, C:], in_=gate[:, C:])
-        cast("S", 0, 0, 2, 304, 384)
-        cast("V", 0, 0, 2, 96, 304)
-        cast("V", 0, 2, 4, 96, 384)
-        cast("S", 0, 0, 4, 0, 96)
-        cast("V", 0, 0, 4, 384, 512)
-        cast("S", 0, 0, 4, 512, 640)
-        quant(0, 0, 256)
-        quant(0, 256, 512)
-        quant(0, 512, 640)
-        cast("S", 1, 0, 2, 128, 384)
-        gather(gwords[0], words[0], 0, 512)
-        cast("S", 1, 0, 4, 0, 128)
-        cast("V", 1, 2, 4, 128, 384)
-        cast("V", 1, 0, 4, 384, 512)
-        cast("S", 1, 0, 4, 512, 640)
-        quant(1, 0, 256)
-        quant(1, 256, 512)
-        quant(1, 512, 640)
-        gather(gplane, plane, 0, 256)
-        gather(gwords[1], words[1], 0, 128)
-        gather(gwords[1], words[1], 128, 256)
-        experts(0)
-        gather(gplane, plane, 256, 512)
-        gather(gwords[1], words[1], 256, 512)
-        experts(1)
+        load_gate(0)
+        load_w8(1)
+        load_w4(1)
+        load_gate(1)
+
+        cast(nc.scalar.copy, 0, 0, 2, FIRST_SPLIT, EARLY)
+        cast(nc.vector.tensor_copy, 0, 0, 2, SCALAR_EARLY, FIRST_SPLIT)
+        finish_pass(0)
+        cast(nc.scalar.copy, 1, 0, 2, SCALAR_EARLY, EARLY)
+        gather(slot_words[0], words[0][:], 0, SLOTS)
+        finish_pass(1)
+
+        gather(slot_scales, scales[:], 0, C)
+        for h in range(2):
+            gather(slot_words[1], words[1][:], HALF * h, HALF * (h + 1))
+        expert(0)
+        gather(slot_scales, scales[:], C, SLOTS)
+        gather(slot_words[1], words[1][:], C, SLOTS)
+        expert(1)
         for e in range(E):
-            scatter(e)
+            places = dst_t[:, C * e // LIST_ROWS : C * (e + 1) // LIST_ROWS]
+            nc.vector.tensor_tensor(out_t[:].indirect(places), y[e][:], gate_t[:, C * e : C * (e + 1)], MULT)
         nc.sync.dma_start(out=out, in_=out_t[:])

@@ -17,6 +17,7 @@ MULT = mybir.AluOpType.mult
 P = 128
 SLOTS = E * C
 HALF = 128
+BANK = 512
 LIST_ROWS = 16
 SCALE_ROW = (4, 0)
 WIDE = T + 64
@@ -54,20 +55,20 @@ def tile_moe_two_lin_gelu_kernel(
         warm = keep.tile([P, 1], F32, name="warm")
 
         def load_pass(a):
-            src = xT[512 * a : 512 * (a + 1), :].rearrange("(p j) t -> p (j t)", j=4)
+            src = xT[4 * P * a : 4 * P * (a + 1), :].rearrange("(p j) t -> p (j t)", j=4)
             for pair in range(2):
                 run = slice(2 * T * pair, 2 * T * pair + T + EARLY)
                 nc.sync.dma_start(out=x_f32[a][:, run], in_=src[:, run])
             nc.sync.dma_start(
-                out=x_f32[a][:].rearrange("p (pair c) -> p pair c", pair=2)[:, :, T + EARLY :],
-                in_=src.rearrange("p (pair c) -> p pair c", pair=2)[:, :, T + EARLY :],
+                out=x_f32[a][:].rearrange("p (pair x) -> p pair x", pair=2)[:, :, T + EARLY :],
+                in_=src.rearrange("p (pair x) -> p pair x", pair=2)[:, :, T + EARLY :],
             )
 
-        def load_w_scales(a, src, quadrants):
-            for q in quadrants:
+        def load_w_scales(a, src):
+            for g in range(4):
                 nc.sync.dma_start(
-                    out=w_scales[32 * q : 32 * q + 4, a, :, :].bitcast(I32),
-                    in_=src[:, 0, 4 * q : 4 * q + 4, :].rearrange("e q n -> q e n").bitcast(I32),
+                    out=w_scales[32 * g : 32 * g + 4, a, :, :].bitcast(I32),
+                    in_=src[:, 0, 4 * g : 4 * g + 4, :].rearrange("e q n -> q e n").bitcast(I32),
                 )
 
         def load_w8(e):
@@ -79,10 +80,10 @@ def tile_moe_two_lin_gelu_kernel(
         def load_gate(e):
             nc.sync.dma_start(out=gate_t[:, C * e : C * (e + 1)], in_=gate[:, C * e : C * (e + 1)])
 
-        def cast(copy, a, j0, j1, s, e):
+        def cast(copy, a, j0, j1, lo, hi):
             copy(
-                x_bf16[a][:, s:e, j0:j1].rearrange("p (c i) j -> p c j i", i=4),
-                x_f32[a][:].rearrange("p (j t) -> p j t", j=4)[:, j0:j1, s:e].rearrange("p j (c i) -> p c j i", i=4),
+                x_bf16[a][:, lo:hi, j0:j1].rearrange("p (c i) j -> p c j i", i=4),
+                x_f32[a][:].rearrange("p (j t) -> p j t", j=4)[:, j0:j1, lo:hi].rearrange("p j (c i) -> p c j i", i=4),
             )
 
         def finish_pass(a):
@@ -90,18 +91,18 @@ def tile_moe_two_lin_gelu_kernel(
             cast(nc.scalar.copy, a, 0, 4, 0, SCALAR_EARLY)
             cast(nc.vector.tensor_copy, a, 0, 4, EARLY, SCALAR_LATE)
             cast(nc.scalar.copy, a, 0, 4, SCALAR_LATE, T)
-            for s, e in QUANT_RANGES:
+            for lo, hi in QUANT_RANGES:
                 nc.vector.quantize_mx(
-                    out=words[a][:, s:e].bitcast(FP8X4),
-                    scales=scales[SCALE_ROW[a] :, s:e],
-                    in_=x_bf16[a][:, s:e, :].rearrange("p t j -> p (t j)"),
+                    out=words[a][:, lo:hi].bitcast(FP8X4),
+                    scales=scales[SCALE_ROW[a] :, lo:hi],
+                    in_=x_bf16[a][:, lo:hi, :].rearrange("p t j -> p (t j)"),
                 )
 
-        def gather(into, window, s, e):
-            nc.vector.tensor_copy(into[:, s:e], window.indirect(offs_t[:, s // LIST_ROWS : e // LIST_ROWS]))
+        def gather(into, window, lo, hi):
+            nc.vector.tensor_copy(into[:, lo:hi], window.indirect(offs_t[:, lo // LIST_ROWS : hi // LIST_ROWS]))
 
         def expert(e):
-            acc = [psum.tile([P, 512], F32, name=f"acc{e}{h}", tag=f"acc{h}") for h in range(2)]
+            acc = [psum.tile([P, BANK], F32, name=f"acc{e}{h}") for h in range(2)]
             for a, w in enumerate((w8[:, e, :].bitcast(FP8X4), w4[:, e, :].bitcast(FP4X4))):
                 for h in range(2):
                     cols = slice(C * e + HALF * h, C * e + HALF * (h + 1))
@@ -127,10 +128,9 @@ def tile_moe_two_lin_gelu_kernel(
         nc.vector.memset(out_t[:], 0.0)
         nc.scalar.activation(warm[:], warm[:], GELU)
         load_w8(0)
-        load_w_scales(0, w8_scales, range(4))
-        load_w_scales(1, w4_scales, range(2))
+        load_w_scales(0, w8_scales)
         load_w4(0)
-        load_w_scales(1, w4_scales, range(2, 4))
+        load_w_scales(1, w4_scales)
         nc.sync.dma_start(out=b_t[:], in_=b)
         nc.sync.dma_start(out=dst_t[:], in_=dst)
         load_gate(0)

@@ -56,13 +56,19 @@ def tile_moe_two_lin_gelu_kernel(
 
         def load_pass(a):
             src = xT[4 * P * a : 4 * P * (a + 1), :].rearrange("(p j) t -> p (j t)", j=4)
-            for pair in range(2):
-                run = slice(2 * T * pair, 2 * T * pair + T + EARLY)
-                nc.sync.dma_start(out=x_f32[a][:, run], in_=src[:, run])
-            nc.sync.dma_start(
-                out=x_f32[a][:].rearrange("p (pair x) -> p pair x", pair=2)[:, :, T + EARLY :],
-                in_=src.rearrange("p (pair x) -> p pair x", pair=2)[:, :, T + EARLY :],
-            )
+            if a == 0:
+                for lo, hi in ((0, T + EARLY), (T + EARLY, 2 * T)):
+                    for pair, queue in enumerate((nc.scalar, nc.sync)):
+                        run = slice(2 * T * pair + lo, 2 * T * pair + hi)
+                        queue.dma_start(out=x_f32[a][:, run], in_=src[:, run])
+            else:
+                for pair in range(2):
+                    run = slice(2 * T * pair, 2 * T * pair + T + EARLY)
+                    nc.sync.dma_start(out=x_f32[a][:, run], in_=src[:, run])
+                nc.sync.dma_start(
+                    out=x_f32[a][:].rearrange("p (pair x) -> p pair x", pair=2)[:, :, T + EARLY :],
+                    in_=src.rearrange("p (pair x) -> p pair x", pair=2)[:, :, T + EARLY :],
+                )
 
         def load_w_scales(a, src):
             for g in range(4):
@@ -86,8 +92,8 @@ def tile_moe_two_lin_gelu_kernel(
                 x_f32[a][:].rearrange("p (j t) -> p j t", j=4)[:, j0:j1, lo:hi].rearrange("p j (c i) -> p c j i", i=4),
             )
 
-        def finish_pass(a):
-            cast(nc.vector.tensor_copy, a, 2, 4, SCALAR_EARLY, EARLY)
+        def finish_pass(a, first_row):
+            cast(nc.vector.tensor_copy, a, first_row, 4, SCALAR_EARLY, EARLY)
             cast(nc.scalar.copy, a, 0, 4, 0, SCALAR_EARLY)
             cast(nc.vector.tensor_copy, a, 0, 4, EARLY, SCALAR_LATE)
             cast(nc.scalar.copy, a, 0, 4, SCALAR_LATE, T)
@@ -133,17 +139,14 @@ def tile_moe_two_lin_gelu_kernel(
         load_w_scales(1, w4_scales)
         nc.sync.dma_start(out=b_t[:], in_=b)
         nc.sync.dma_start(out=dst_t[:], in_=dst)
-        load_gate(0)
+        nc.sync.dma_start(out=gate_t[:], in_=gate)
         load_w8(1)
         load_w4(1)
-        load_gate(1)
 
-        cast(nc.scalar.copy, 0, 0, 2, FIRST_SPLIT, EARLY)
-        cast(nc.vector.tensor_copy, 0, 0, 2, SCALAR_EARLY, FIRST_SPLIT)
-        finish_pass(0)
+        finish_pass(0, 0)
         cast(nc.scalar.copy, 1, 0, 2, SCALAR_EARLY, EARLY)
         gather(slot_words[0], words[0][:], 0, SLOTS)
-        finish_pass(1)
+        finish_pass(1, 2)
 
         gather(slot_scales, scales[:], 0, C)
         for h in range(2):

@@ -23,9 +23,8 @@ SCALE_ROW = (4, 0)
 WIDE = T + 64
 
 EARLY = 384
-SCALAR_EARLY = 128
+SCALAR_EARLY = 152
 SCALAR_LATE = 512
-FIRST_SPLIT = 304
 QUANT_RANGES = ((0, 256), (256, SCALAR_LATE), (SCALAR_LATE, T))
 
 
@@ -54,21 +53,18 @@ def tile_moe_two_lin_gelu_kernel(
         out_t = keep.tile([P, T], F32, name="out_t")
         warm = keep.tile([P, 1], F32, name="warm")
 
-        def load_pass(a):
-            src = xT[4 * P * a : 4 * P * (a + 1), :].rearrange("(p j) t -> p (j t)", j=4)
-            if a == 0:
-                for lo, hi in ((0, T + EARLY), (T + EARLY, 2 * T)):
-                    for pair, queue in enumerate((nc.scalar, nc.sync)):
-                        run = slice(2 * T * pair + lo, 2 * T * pair + hi)
-                        queue.dma_start(out=x_f32[a][:, run], in_=src[:, run])
-            else:
-                for pair in range(2):
-                    run = slice(2 * T * pair, 2 * T * pair + T + EARLY)
-                    nc.sync.dma_start(out=x_f32[a][:, run], in_=src[:, run])
-                nc.sync.dma_start(
-                    out=x_f32[a][:].rearrange("p (pair x) -> p pair x", pair=2)[:, :, T + EARLY :],
-                    in_=src.rearrange("p (pair x) -> p pair x", pair=2)[:, :, T + EARLY :],
-                )
+        def x_rows(a):
+            return xT[4 * P * a : 4 * P * (a + 1), :].rearrange("(p j) t -> p (j t)", j=4)
+
+        def load_run(queue, a, pair, lo, hi):
+            run = slice(2 * T * pair + lo, 2 * T * pair + hi)
+            queue.dma_start(out=x_f32[a][:, run], in_=x_rows(a)[:, run])
+
+        def load_tails(a):
+            nc.sync.dma_start(
+                out=x_f32[a][:].rearrange("p (pair x) -> p pair x", pair=2)[:, :, T + EARLY :],
+                in_=x_rows(a).rearrange("p (pair x) -> p pair x", pair=2)[:, :, T + EARLY :],
+            )
 
         def load_w_scales(a, src):
             for g in range(4):
@@ -82,9 +78,6 @@ def tile_moe_two_lin_gelu_kernel(
 
         def load_w4(e):
             nc.sync.dma_start(out=w4[:, e, :].bitcast(I32), in_=w4_words[e, 0].bitcast(I32))
-
-        def load_gate(e):
-            nc.sync.dma_start(out=gate_t[:, C * e : C * (e + 1)], in_=gate[:, C * e : C * (e + 1)])
 
         def cast(copy, a, j0, j1, lo, hi):
             copy(
@@ -124,9 +117,13 @@ def tile_moe_two_lin_gelu_kernel(
             for h in range(2):
                 nc.scalar.activation(y[e][:, HALF * h : HALF * (h + 1)], acc[h][:, :HALF], GELU, bias=b_t[:, e : e + 1])
 
-        load_pass(0)
+        for lo, hi in ((0, T + EARLY), (T + EARLY, 2 * T)):
+            for pair, queue in enumerate((nc.scalar, nc.sync)):
+                load_run(queue, 0, pair, lo, hi)
         nc.sync.dma_start(out=offs_t[:], in_=offs)
-        load_pass(1)
+        for pair in range(2):
+            load_run(nc.sync, 1, pair, 0, T + EARLY)
+        load_tails(1)
         nc.vector.memset(w_scales[:].rearrange("p a e n -> p (a e n)").bitcast(I32), 0)
         nc.vector.memset(warm[:], 0.0)
         nc.vector.memset(words[0][:, T:].bitcast(I32), 0)
@@ -143,10 +140,10 @@ def tile_moe_two_lin_gelu_kernel(
         load_w8(1)
         load_w4(1)
 
-        finish_pass(0, 0)
+        finish_pass(0, first_row=0)
         cast(nc.scalar.copy, 1, 0, 2, SCALAR_EARLY, EARLY)
         gather(slot_words[0], words[0][:], 0, SLOTS)
-        finish_pass(1, 2)
+        finish_pass(1, first_row=2)
 
         gather(slot_scales, scales[:], 0, C)
         for h in range(2):

@@ -38,9 +38,9 @@ def tile_moe_two_lin_gelu_kernel(
     ):
         offs_t = keep.tile([P, SLOTS // LIST_ROWS], U16, name="offs_t")
         dst_t = keep.tile([P, SLOTS // LIST_ROWS], U16, name="dst_t")
-        x_f32 = [keep.tile([P, 4 * T], F32, name=f"x_f32_{a}", align_bytes=64) for a in range(2)]
+        x_f32 = [keep.tile([P, 4 * T], F32, name=f"x_f32_{a}", tag=f"x_f32_{a}", align_bytes=64) for a in range(2)]
         x_bf16 = [keep.tile([P, T, 4], BF16, name=f"x_bf16_{a}", align_bytes=64) for a in range(2)]
-        words = [keep.tile([P, width], U32, name=f"words{a}", align_bytes=64) for a, width in enumerate((WIDE, T))]
+        words = [keep.tile([P, width], U32, name=f"words{a}", align_bytes=64) for a, width in enumerate((T, T))]
         scales = keep.tile([P, T], U8, name="scales", align_bytes=64)
         slot_words = [keep.tile([P, SLOTS], U32, name=f"slot_words{a}", align_bytes=64) for a in range(2)]
         slot_scales = keep.tile([P, SLOTS], U8, name="slot_scales", align_bytes=64)
@@ -109,7 +109,7 @@ def tile_moe_two_lin_gelu_kernel(
                         out=acc[h][:, :HALF],
                         lhsT=w,
                         lhsT_scale=w_scales[:, a, e, :],
-                        rhs=slot_words[a][:, cols].bitcast(FP8X4),
+                        rhs=(last_words[:] if (a, e, h) == (0, 1, 1) else slot_words[a][:, cols]).bitcast(FP8X4),
                         rhs_scale=slot_scales[SCALE_ROW[a] :, cols],
                         start=(a == 0),
                         stop=(a == 1),
@@ -126,7 +126,6 @@ def tile_moe_two_lin_gelu_kernel(
         load_tails(1)
         nc.vector.memset(w_scales[:].rearrange("p a e n -> p (a e n)").bitcast(I32), 0)
         nc.vector.memset(warm[:], 0.0)
-        nc.vector.memset(words[0][:, T:].bitcast(I32), 0)
         nc.vector.memset(scales[:].bitcast(I32), 0)
         nc.vector.memset(out_t[:], 0.0)
         nc.scalar.activation(warm[:], warm[:], GELU)
@@ -142,8 +141,10 @@ def tile_moe_two_lin_gelu_kernel(
 
         finish_pass(0, first_row=0)
         cast(nc.scalar.copy, 1, 0, 2, SCALAR_EARLY, EARLY)
-        gather(slot_words[0], words[0][:], 0, SLOTS)
+        gather(slot_words[0], words[0][:], 0, SLOTS - HALF)
         finish_pass(1, first_row=2)
+        last_words = keep.tile([P, HALF], U32, name="last_words", tag="x_f32_1", align_bytes=64)
+        nc.vector.tensor_copy(last_words[:], words[0][:].indirect(offs_t[:, (SLOTS - HALF) // LIST_ROWS :]))
 
         gather(slot_scales, scales[:], 0, C)
         for h in range(2):

@@ -20,12 +20,15 @@ HALF = 128
 BANK = 512
 LIST_ROWS = 16
 SCALE_ROW = (4, 0)
-WIDE = T + 64
+LAST_HALF = SLOTS - HALF
 
 EARLY = 384
-SCALAR_EARLY = 152
+SCALAR_EARLY_0 = 152
+SCALAR_EARLY_1 = 240
 SCALAR_LATE = 512
-QUANT_RANGES = ((0, 256), (256, SCALAR_LATE), (SCALAR_LATE, T))
+AHEAD = 128
+QUANT_RANGES_0 = ((0, 256), (256, SCALAR_LATE), (SCALAR_LATE, T))
+QUANT_RANGES_1 = ((AHEAD, EARLY), (EARLY, SCALAR_LATE), (SCALAR_LATE, T))
 
 
 def tile_moe_two_lin_gelu_kernel(
@@ -40,7 +43,7 @@ def tile_moe_two_lin_gelu_kernel(
         dst_t = keep.tile([P, SLOTS // LIST_ROWS], U16, name="dst_t")
         x_f32 = [keep.tile([P, 4 * T], F32, name=f"x_f32_{a}", tag=f"x_f32_{a}", align_bytes=64) for a in range(2)]
         x_bf16 = [keep.tile([P, T, 4], BF16, name=f"x_bf16_{a}", align_bytes=64) for a in range(2)]
-        words = [keep.tile([P, width], U32, name=f"words{a}", align_bytes=64) for a, width in enumerate((T, T))]
+        words = [keep.tile([P, T], U32, name=f"words{a}", align_bytes=64) for a in range(2)]
         scales = keep.tile([P, T], U8, name="scales", align_bytes=64)
         slot_words = [keep.tile([P, SLOTS], U32, name=f"slot_words{a}", align_bytes=64) for a in range(2)]
         slot_scales = keep.tile([P, SLOTS], U8, name="slot_scales", align_bytes=64)
@@ -85,17 +88,16 @@ def tile_moe_two_lin_gelu_kernel(
                 x_f32[a][:].rearrange("p (j t) -> p j t", j=4)[:, j0:j1, lo:hi].rearrange("p j (c i) -> p c j i", i=4),
             )
 
-        def finish_pass(a, first_row):
-            cast(nc.vector.tensor_copy, a, first_row, 4, SCALAR_EARLY, EARLY)
-            cast(nc.scalar.copy, a, 0, 4, 0, SCALAR_EARLY)
+        def quantize(a, lo, hi):
+            nc.vector.quantize_mx(
+                out=words[a][:, lo:hi].bitcast(FP8X4),
+                scales=scales[SCALE_ROW[a] :, lo:hi],
+                in_=x_bf16[a][:, lo:hi, :].rearrange("p t j -> p (t j)"),
+            )
+
+        def cast_late(a):
             cast(nc.vector.tensor_copy, a, 0, 4, EARLY, SCALAR_LATE)
             cast(nc.scalar.copy, a, 0, 4, SCALAR_LATE, T)
-            for lo, hi in QUANT_RANGES:
-                nc.vector.quantize_mx(
-                    out=words[a][:, lo:hi].bitcast(FP8X4),
-                    scales=scales[SCALE_ROW[a] :, lo:hi],
-                    in_=x_bf16[a][:, lo:hi, :].rearrange("p t j -> p (t j)"),
-                )
 
         def gather(into, window, lo, hi):
             nc.vector.tensor_copy(into[:, lo:hi], window.indirect(offs_t[:, lo // LIST_ROWS : hi // LIST_ROWS]))
@@ -105,11 +107,12 @@ def tile_moe_two_lin_gelu_kernel(
             for a, w in enumerate((w8[:, e, :].bitcast(FP8X4), w4[:, e, :].bitcast(FP4X4))):
                 for h in range(2):
                     cols = slice(C * e + HALF * h, C * e + HALF * (h + 1))
+                    moving = last_words[:] if (a, cols.start) == (0, LAST_HALF) else slot_words[a][:, cols]
                     nc.tensor.matmul_mx(
                         out=acc[h][:, :HALF],
                         lhsT=w,
                         lhsT_scale=w_scales[:, a, e, :],
-                        rhs=(last_words[:] if (a, e, h) == (0, 1, 1) else slot_words[a][:, cols]).bitcast(FP8X4),
+                        rhs=moving.bitcast(FP8X4),
                         rhs_scale=slot_scales[SCALE_ROW[a] :, cols],
                         start=(a == 0),
                         stop=(a == 1),
@@ -139,12 +142,22 @@ def tile_moe_two_lin_gelu_kernel(
         load_w8(1)
         load_w4(1)
 
-        finish_pass(0, first_row=0)
-        cast(nc.scalar.copy, 1, 0, 2, SCALAR_EARLY, EARLY)
-        gather(slot_words[0], words[0][:], 0, SLOTS - HALF)
-        finish_pass(1, first_row=2)
+        cast(nc.vector.tensor_copy, 0, 0, 4, SCALAR_EARLY_0, EARLY)
+        cast(nc.scalar.copy, 0, 0, 4, 0, SCALAR_EARLY_0)
+        cast_late(0)
+        for lo, hi in QUANT_RANGES_0:
+            quantize(0, lo, hi)
+        cast(nc.scalar.copy, 1, 0, 2, 0, SCALAR_EARLY_1)
+        gather(slot_words[0], words[0][:], 0, LAST_HALF)
+        cast(nc.vector.tensor_copy, 1, 2, 4, 0, AHEAD)
+        cast(nc.vector.tensor_copy, 1, 2, 4, AHEAD, SCALAR_EARLY_1)
+        cast(nc.scalar.copy, 1, 0, 4, SCALAR_EARLY_1, EARLY)
+        quantize(1, 0, AHEAD)
+        cast_late(1)
+        for lo, hi in QUANT_RANGES_1:
+            quantize(1, lo, hi)
         last_words = keep.tile([P, HALF], U32, name="last_words", tag="x_f32_1", align_bytes=64)
-        nc.vector.tensor_copy(last_words[:], words[0][:].indirect(offs_t[:, (SLOTS - HALF) // LIST_ROWS :]))
+        nc.vector.tensor_copy(last_words[:], words[0][:].indirect(offs_t[:, LAST_HALF // LIST_ROWS :]))
 
         gather(slot_scales, scales[:], 0, C)
         for h in range(2):

@@ -12,23 +12,15 @@ U8 = mybir.dt.uint8
 FP8X4 = mybir.dt.float8_e4m3fn_x4
 FP4X4 = mybir.dt.float4_e2m1fn_x4
 GELU = mybir.ActivationFunctionType.Gelu_apprx_tanh
+COPY = mybir.ActivationFunctionType.Copy
 MULT = mybir.AluOpType.mult
+ADD = mybir.AluOpType.add
 
 P = 128
 SLOTS = E * C
-HALF = 128
+CHUNK = 128
 BANK = 512
 LIST_ROWS = 16
-SCALE_ROW = (4, 0)
-LAST_HALF = SLOTS - HALF
-
-EARLY = 384
-SCALAR_EARLY_0 = 152
-SCALAR_EARLY_1 = 240
-SCALAR_LATE = 512
-AHEAD = 128
-QUANT_RANGES_0 = ((0, 256), (256, SCALAR_LATE), (SCALAR_LATE, T))
-QUANT_RANGES_1 = ((AHEAD, EARLY), (EARLY, SCALAR_LATE), (SCALAR_LATE, T))
 
 
 def tile_moe_two_lin_gelu_kernel(
@@ -41,132 +33,139 @@ def tile_moe_two_lin_gelu_kernel(
     ):
         offs_t = keep.tile([P, SLOTS // LIST_ROWS], U16, name="offs_t")
         dst_t = keep.tile([P, SLOTS // LIST_ROWS], U16, name="dst_t")
-        x_f32 = [keep.tile([P, 4 * T], F32, name=f"x_f32_{a}", tag=f"x_f32_{a}", align_bytes=64) for a in range(2)]
-        x_bf16 = [keep.tile([P, T, 4], BF16, name=f"x_bf16_{a}", align_bytes=64) for a in range(2)]
-        words = [keep.tile([P, T], U32, name=f"words{a}", align_bytes=64) for a in range(2)]
-        scales = keep.tile([P, T], U8, name="scales", align_bytes=64)
-        slot_words = [keep.tile([P, SLOTS], U32, name=f"slot_words{a}", align_bytes=64) for a in range(2)]
-        slot_scales = keep.tile([P, SLOTS], U8, name="slot_scales", align_bytes=64)
+        rows = [[keep.tile([P, T], F32, name=f"row{a}{j}", align_bytes=64) for j in range(4)] for a in range(2)]
+        planes = [keep.tile([P, 4 * SLOTS], BF16, name=f"planes{a}", align_bytes=64) for a in range(2)]
+        woven = [keep.tile([P, SLOTS, 4], BF16, name=f"woven{a}", align_bytes=64) for a in range(2)]
+        words = [keep.tile([P, SLOTS], U32, name=f"words{a}", align_bytes=64) for a in range(2)]
+        scales = [keep.tile([P, SLOTS], U8, name=f"scales{a}", align_bytes=64) for a in range(2)]
         w8 = keep.tile([P, E, 4 * N], U8, name="w8", align_bytes=64)
         w4 = keep.tile([P, E, 2 * N], U8, name="w4", align_bytes=64)
         w_scales = keep.tile([P, 2, E, N], U8, name="w_scales", align_bytes=64)
         b_t = keep.tile([P, E], F32, name="b_t")
         gate_t = keep.tile([P, SLOTS], F32, name="gate_t")
-        y = [keep.tile([P, C], F32, name=f"y{e}") for e in range(E)]
+        y = keep.tile([P, SLOTS], F32, name="y")
+        gated = keep.tile([P, SLOTS], F32, name="gated")
+        by_vector = keep.tile([P, T], F32, name="by_vector")
+        by_scalar = keep.tile([P, T], F32, name="by_scalar")
         out_t = keep.tile([P, T], F32, name="out_t")
         warm = keep.tile([P, 1], F32, name="warm")
+        acc = [psum.tile([P, BANK], F32, name=f"acc{c}") for c in range(SLOTS // CHUNK)]
 
-        def x_rows(a):
-            return xT[4 * P * a : 4 * P * (a + 1), :].rearrange("(p j) t -> p (j t)", j=4)
+        def entries(list_t, lo, hi):
+            return list_t[:, lo // LIST_ROWS : hi // LIST_ROWS]
 
-        def load_run(queue, a, pair, lo, hi):
-            run = slice(2 * T * pair + lo, 2 * T * pair + hi)
-            queue.dma_start(out=x_f32[a][:, run], in_=x_rows(a)[:, run])
-
-        def load_tails(a):
-            nc.sync.dma_start(
-                out=x_f32[a][:].rearrange("p (pair x) -> p pair x", pair=2)[:, :, T + EARLY :],
-                in_=x_rows(a).rearrange("p (pair x) -> p pair x", pair=2)[:, :, T + EARLY :],
+        def gather_v(a, j, lo, hi):
+            nc.vector.tensor_copy(
+                planes[a][:, SLOTS * j + lo : SLOTS * j + hi], rows[a][j][:].indirect(entries(offs_t, lo, hi))
             )
 
-        def load_w_scales(a, src):
-            for g in range(4):
-                nc.sync.dma_start(
-                    out=w_scales[32 * g : 32 * g + 4, a, :, :].bitcast(I32),
-                    in_=src[:, 0, 4 * g : 4 * g + 4, :].rearrange("e q n -> q e n").bitcast(I32),
-                )
+        def gather_s(a, j, lo, hi):
+            nc.scalar.activation(
+                planes[a][:, SLOTS * j + lo : SLOTS * j + hi], rows[a][j][:].indirect(entries(offs_t, lo, hi)), COPY
+            )
 
-        def load_w8(e):
-            nc.sync.dma_start(out=w8[:, e, :].bitcast(I32), in_=w8_words[e, 0].rearrange("p n r -> p (n r)").bitcast(I32))
-
-        def load_w4(e):
-            nc.sync.dma_start(out=w4[:, e, :].bitcast(I32), in_=w4_words[e, 0].bitcast(I32))
-
-        def cast(copy, a, j0, j1, lo, hi):
-            copy(
-                x_bf16[a][:, lo:hi, j0:j1].rearrange("p (c i) j -> p c j i", i=4),
-                x_f32[a][:].rearrange("p (j t) -> p j t", j=4)[:, j0:j1, lo:hi].rearrange("p j (c i) -> p c j i", i=4),
+        def weave(a, lo, hi):
+            nc.vector.tensor_copy(
+                woven[a][:, lo:hi, :].rearrange("p (c i) j -> p c j i", i=4),
+                planes[a][:].rearrange("p (j s) -> p j s", j=4)[:, :, lo:hi].rearrange("p j (c i) -> p c j i", i=4),
             )
 
         def quantize(a, lo, hi):
             nc.vector.quantize_mx(
                 out=words[a][:, lo:hi].bitcast(FP8X4),
-                scales=scales[SCALE_ROW[a] :, lo:hi],
-                in_=x_bf16[a][:, lo:hi, :].rearrange("p t j -> p (t j)"),
+                scales=scales[a][:, lo:hi],
+                in_=woven[a][:, lo:hi, :].rearrange("p t j -> p (t j)"),
             )
 
-        def cast_late(a):
-            cast(nc.vector.tensor_copy, a, 0, 4, EARLY, SCALAR_LATE)
-            cast(nc.scalar.copy, a, 0, 4, SCALAR_LATE, T)
+        def matmul(a, c):
+            e = CHUNK * c // C
+            cols = slice(CHUNK * c, CHUNK * (c + 1))
+            w = w8[:, e, :].bitcast(FP8X4) if a == 0 else w4[:, e, :].bitcast(FP4X4)
+            nc.tensor.matmul_mx(
+                out=acc[c][:, :CHUNK],
+                lhsT=w,
+                lhsT_scale=w_scales[:, a, e, :],
+                rhs=words[a][:, cols].bitcast(FP8X4),
+                rhs_scale=scales[a][:, cols],
+                start=(a == 0),
+                stop=(a == 1),
+            )
 
-        def gather(into, window, lo, hi):
-            nc.vector.tensor_copy(into[:, lo:hi], window.indirect(offs_t[:, lo // LIST_ROWS : hi // LIST_ROWS]))
+        def finish(c):
+            e = CHUNK * c // C
+            matmul(1, c)
+            nc.scalar.activation(y[:, CHUNK * c : CHUNK * (c + 1)], acc[c][:, :CHUNK], GELU, bias=b_t[:, e : e + 1])
 
-        def expert(e):
-            acc = [psum.tile([P, BANK], F32, name=f"acc{e}{h}") for h in range(2)]
-            for a, w in enumerate((w8[:, e, :].bitcast(FP8X4), w4[:, e, :].bitcast(FP4X4))):
-                for h in range(2):
-                    cols = slice(C * e + HALF * h, C * e + HALF * (h + 1))
-                    moving = last_words[:] if (a, cols.start) == (0, LAST_HALF) else slot_words[a][:, cols]
-                    nc.tensor.matmul_mx(
-                        out=acc[h][:, :HALF],
-                        lhsT=w,
-                        lhsT_scale=w_scales[:, a, e, :],
-                        rhs=moving.bitcast(FP8X4),
-                        rhs_scale=slot_scales[SCALE_ROW[a] :, cols],
-                        start=(a == 0),
-                        stop=(a == 1),
-                    )
-            for h in range(2):
-                nc.scalar.activation(y[e][:, HALF * h : HALF * (h + 1)], acc[h][:, :HALF], GELU, bias=b_t[:, e : e + 1])
+        def times_gate(lo, hi):
+            nc.vector.tensor_tensor(gated[:, lo:hi], y[:, lo:hi], gate_t[:, lo:hi], MULT)
 
-        for lo, hi in ((0, T + EARLY), (T + EARLY, 2 * T)):
-            for pair, queue in enumerate((nc.scalar, nc.sync)):
-                load_run(queue, 0, pair, lo, hi)
-        nc.sync.dma_start(out=offs_t[:], in_=offs)
-        for pair in range(2):
-            load_run(nc.sync, 1, pair, 0, T + EARLY)
-        load_tails(1)
+        def scatter_s(lo, hi):
+            nc.scalar.activation(by_scalar[:].indirect(entries(dst_t, lo, hi)), gated[:, lo:hi], COPY)
+
+        def scatter_v(lo, hi):
+            nc.vector.tensor_tensor(by_vector[:].indirect(entries(dst_t, lo, hi)), y[:, lo:hi], gate_t[:, lo:hi], MULT)
+
+        def load_w_scales(a, src, g):
+            nc.sync.dma_start(
+                out=w_scales[32 * g : 32 * g + 4, a, :, :].bitcast(I32),
+                in_=src[:, 0, 4 * g : 4 * g + 4, :].rearrange("e q n -> q e n").bitcast(I32),
+            )
+
+        def load_row(a, j):
+            nc.sync.dma_start(
+                out=rows[a][j][:], in_=xT[4 * P * a : 4 * P * (a + 1), :].rearrange("(p j) t -> p j t", j=4)[:, j, :]
+            )
+
         nc.vector.memset(w_scales[:].rearrange("p a e n -> p (a e n)").bitcast(I32), 0)
+        nc.sync.dma_start(out=offs_t[:], in_=offs)
+        for j in range(4):
+            load_row(0, j)
+        for j in range(4):
+            load_w_scales(0, w8_scales, j)
+            load_row(1, j)
         nc.vector.memset(warm[:], 0.0)
-        nc.vector.memset(scales[:].bitcast(I32), 0)
-        nc.vector.memset(out_t[:], 0.0)
+        nc.vector.memset(by_vector[:], 0.0)
+        nc.vector.memset(by_scalar[:], 0.0)
         nc.scalar.activation(warm[:], warm[:], GELU)
-        load_w8(0)
-        load_w_scales(0, w8_scales)
-        load_w4(0)
-        load_w_scales(1, w4_scales)
+        nc.sync.dma_start(out=w8[:].bitcast(I32), in_=w8_words[:, 0].rearrange("e p n r -> p e (n r)").bitcast(I32))
+        nc.sync.dma_start(out=w4[:].bitcast(I32), in_=w4_words[:, 0].rearrange("e p x -> p e x").bitcast(I32))
+        nc.sync.dma_start(out=gate_t[:], in_=gate)
+        for g in range(4):
+            load_w_scales(1, w4_scales, g)
         nc.sync.dma_start(out=b_t[:], in_=b)
         nc.sync.dma_start(out=dst_t[:], in_=dst)
-        nc.sync.dma_start(out=gate_t[:], in_=gate)
-        load_w8(1)
-        load_w4(1)
 
-        cast(nc.vector.tensor_copy, 0, 0, 4, SCALAR_EARLY_0, EARLY)
-        cast(nc.scalar.copy, 0, 0, 4, 0, SCALAR_EARLY_0)
-        cast_late(0)
-        for lo, hi in QUANT_RANGES_0:
-            quantize(0, lo, hi)
-        cast(nc.scalar.copy, 1, 0, 2, 0, SCALAR_EARLY_1)
-        gather(slot_words[0], words[0][:], 0, LAST_HALF)
-        cast(nc.vector.tensor_copy, 1, 2, 4, 0, AHEAD)
-        cast(nc.vector.tensor_copy, 1, 2, 4, AHEAD, SCALAR_EARLY_1)
-        cast(nc.scalar.copy, 1, 0, 4, SCALAR_EARLY_1, EARLY)
-        quantize(1, 0, AHEAD)
-        cast_late(1)
-        for lo, hi in QUANT_RANGES_1:
-            quantize(1, lo, hi)
-        last_words = keep.tile([P, HALF], U32, name="last_words", tag="x_f32_1", align_bytes=64)
-        nc.vector.tensor_copy(last_words[:], words[0][:].indirect(offs_t[:, LAST_HALF // LIST_ROWS :]))
-
-        gather(slot_scales, scales[:], 0, C)
-        for h in range(2):
-            gather(slot_words[1], words[1][:], HALF * h, HALF * (h + 1))
-        expert(0)
-        gather(slot_scales, scales[:], C, SLOTS)
-        gather(slot_words[1], words[1][:], C, SLOTS)
-        expert(1)
+        for j in range(4):
+            gather_v(0, j, 0, C)
+            gather_s(0, j, C, SLOTS)
         for e in range(E):
-            places = dst_t[:, C * e // LIST_ROWS : C * (e + 1) // LIST_ROWS]
-            nc.vector.tensor_tensor(out_t[:].indirect(places), y[e][:], gate_t[:, C * e : C * (e + 1)], MULT)
-        nc.sync.dma_start(out=out, in_=out_t[:])
+            weave(0, C * e, C * (e + 1))
+        for e in range(E):
+            quantize(0, C * e, C * (e + 1))
+        for c in range(4):
+            matmul(0, c)
+        for j in range(2):
+            for e in range(E):
+                gather_s(1, j, C * e, C * (e + 1))
+        gather_v(1, 2, 0, 256)
+        gather_v(1, 3, 0, 128)
+        gather_s(1, 3, 128, 256)
+        for c in range(2, 4):
+            for j in range(2, 4):
+                gather_s(1, j, CHUNK * c, CHUNK * (c + 1))
+        for pair in range(2):
+            for c in (2 * pair, 2 * pair + 1):
+                weave(1, CHUNK * c, CHUNK * (c + 1))
+            for c in (2 * pair, 2 * pair + 1):
+                quantize(1, CHUNK * c, CHUNK * (c + 1))
+                finish(c)
+            if pair == 0:
+                times_gate(0, 128)
+                scatter_s(0, 128)
+        scatter_v(128, 256)
+        times_gate(256, 384)
+        scatter_s(256, 384)
+        scatter_v(384, 512)
+        for cols in (slice(0, T // 2), slice(T // 2, T)):
+            nc.vector.tensor_tensor(out_t[:, cols], by_vector[:, cols], by_scalar[:, cols], ADD)
+            nc.sync.dma_start(out=out[:, cols], in_=out_t[:, cols])

@@ -21,6 +21,7 @@ SLOTS = E * C
 CHUNK = 128
 BANK = 512
 LIST_ROWS = 16
+WIDE = 2 * SLOTS
 
 
 def tile_moe_two_lin_gelu_kernel(
@@ -33,7 +34,10 @@ def tile_moe_two_lin_gelu_kernel(
     ):
         offs_t = keep.tile([P, SLOTS // LIST_ROWS], U16, name="offs_t")
         dst_t = keep.tile([P, SLOTS // LIST_ROWS], U16, name="dst_t")
-        rows = [[keep.tile([P, T], F32, name=f"row{a}{j}", align_bytes=64) for j in range(4)] for a in range(2)]
+        rows = [
+            [keep.tile([P, WIDE if (a, j) in ((1, 0), (1, 1)) else T], F32, name=f"row{a}{j}", align_bytes=64) for j in range(4)]
+            for a in range(2)
+        ]
         planes = [keep.tile([P, 4 * SLOTS], BF16, name=f"planes{a}", align_bytes=64) for a in range(2)]
         woven = [keep.tile([P, SLOTS, 4], BF16, name=f"woven{a}", align_bytes=64) for a in range(2)]
         words = [keep.tile([P, SLOTS], U32, name=f"words{a}", align_bytes=64) for a in range(2)]
@@ -64,8 +68,8 @@ def tile_moe_two_lin_gelu_kernel(
                 planes[a][:, SLOTS * j + lo : SLOTS * j + hi], rows[a][j][:].indirect(entries(offs_t, lo, hi)), COPY
             )
 
-        def weave(a, lo, hi):
-            nc.vector.tensor_copy(
+        def weave(a, lo, hi, copy=nc.vector.tensor_copy):
+            copy(
                 woven[a][:, lo:hi, :].rearrange("p (c i) j -> p c j i", i=4),
                 planes[a][:].rearrange("p (j s) -> p j s", j=4)[:, :, lo:hi].rearrange("p j (c i) -> p c j i", i=4),
             )
@@ -113,7 +117,7 @@ def tile_moe_two_lin_gelu_kernel(
 
         def load_row(a, j):
             nc.sync.dma_start(
-                out=rows[a][j][:], in_=xT[4 * P * a : 4 * P * (a + 1), :].rearrange("(p j) t -> p j t", j=4)[:, j, :]
+                out=rows[a][j][:, :T], in_=xT[4 * P * a : 4 * P * (a + 1), :].rearrange("(p j) t -> p j t", j=4)[:, j, :]
             )
 
         nc.vector.memset(w_scales[:].rearrange("p a e n -> p (a e n)").bitcast(I32), 0)
@@ -128,10 +132,10 @@ def tile_moe_two_lin_gelu_kernel(
         nc.vector.memset(by_scalar[:], 0.0)
         nc.scalar.activation(warm[:], warm[:], GELU)
         nc.sync.dma_start(out=w8[:].bitcast(I32), in_=w8_words[:, 0].rearrange("e p n r -> p e (n r)").bitcast(I32))
-        nc.sync.dma_start(out=w4[:].bitcast(I32), in_=w4_words[:, 0].rearrange("e p x -> p e x").bitcast(I32))
-        nc.sync.dma_start(out=gate_t[:], in_=gate)
         for g in range(4):
             load_w_scales(1, w4_scales, g)
+        nc.sync.dma_start(out=w4[:].bitcast(I32), in_=w4_words[:, 0].rearrange("e p x -> p e x").bitcast(I32))
+        nc.sync.dma_start(out=gate_t[:], in_=gate)
         nc.sync.dma_start(out=b_t[:], in_=b)
         nc.sync.dma_start(out=dst_t[:], in_=dst)
 
@@ -145,27 +149,25 @@ def tile_moe_two_lin_gelu_kernel(
         for c in range(4):
             matmul(0, c)
         for j in range(2):
-            for e in range(E):
-                gather_s(1, j, C * e, C * (e + 1))
+            gather_s(1, j, 0, SLOTS)
         gather_v(1, 2, 0, 256)
         gather_v(1, 3, 0, 128)
-        gather_s(1, 3, 128, 256)
-        for c in range(2, 4):
-            for j in range(2, 4):
-                gather_s(1, j, CHUNK * c, CHUNK * (c + 1))
+        gather_v(1, 3, 128, 256)
+        gather_s(1, 2, 256, 512)
+        gather_s(1, 3, 256, 384)
+        gather_s(1, 3, 384, 512)
         for pair in range(2):
             for c in (2 * pair, 2 * pair + 1):
-                weave(1, CHUNK * c, CHUNK * (c + 1))
+                weave(1, CHUNK * c, CHUNK * (c + 1), nc.scalar.copy if c == 3 else nc.vector.tensor_copy)
             for c in (2 * pair, 2 * pair + 1):
                 quantize(1, CHUNK * c, CHUNK * (c + 1))
                 finish(c)
-            if pair == 0:
-                times_gate(0, 128)
-                scatter_s(0, 128)
+        times_gate(0, 128)
+        scatter_s(0, 128)
         scatter_v(128, 256)
-        times_gate(256, 384)
-        scatter_s(256, 384)
-        scatter_v(384, 512)
+        times_gate(256, 352)
+        scatter_s(256, 352)
+        scatter_v(352, 512)
         for cols in (slice(0, T // 2), slice(T // 2, T)):
             nc.vector.tensor_tensor(out_t[:, cols], by_vector[:, cols], by_scalar[:, cols], ADD)
             nc.sync.dma_start(out=out[:, cols], in_=out_t[:, cols])

@@ -140,25 +140,25 @@ def tile_moe_two_lin_gelu_kernel(
         nc.sync.dma_start(out=dst_t[:], in_=dst)
 
         for j in range(4):
-            gather_v(0, j, 0, C)
+            for lo, hi in ((0, CHUNK), (CHUNK, C)) if j == 3 else ((0, C),):
+                gather_v(0, j, lo, hi)
             gather_s(0, j, C, SLOTS)
-        for e in range(E):
-            weave(0, C * e, C * (e + 1))
-        for e in range(E):
-            quantize(0, C * e, C * (e + 1))
+        for step in (weave, quantize):
+            step(0, 0, CHUNK)
+            step(0, CHUNK, SLOTS)
         for c in range(4):
             matmul(0, c)
         for j in range(2):
             gather_s(1, j, 0, SLOTS)
-        gather_v(1, 2, 0, 256)
+        gather_v(1, 2, 0, 192)
         gather_v(1, 3, 0, 128)
         gather_v(1, 3, 128, 256)
-        gather_s(1, 2, 256, 512)
+        gather_s(1, 2, 192, 512)
         gather_s(1, 3, 256, 384)
         gather_s(1, 3, 384, 512)
         for pair in range(2):
             for c in (2 * pair, 2 * pair + 1):
-                weave(1, CHUNK * c, CHUNK * (c + 1), nc.scalar.copy if c == 3 else nc.vector.tensor_copy)
+                weave(1, CHUNK * c, CHUNK * (c + 1))
             for c in (2 * pair, 2 * pair + 1):
                 quantize(1, CHUNK * c, CHUNK * (c + 1))
                 finish(c)

@@ -39,6 +39,7 @@ def tile_moe_two_lin_gelu_kernel(
             for a in range(2)
         ]
         planes = [keep.tile([P, 4 * SLOTS], BF16, name=f"planes{a}", align_bytes=64) for a in range(2)]
+        pairs = keep.tile([P, 2, C, 2], BF16, name="pairs", align_bytes=64)
         woven = [keep.tile([P, SLOTS, 4], BF16, name=f"woven{a}", align_bytes=64) for a in range(2)]
         words = [keep.tile([P, SLOTS], U32, name=f"words{a}", align_bytes=64) for a in range(2)]
         scales = [keep.tile([P, SLOTS], U8, name=f"scales{a}", align_bytes=64) for a in range(2)]
@@ -61,6 +62,15 @@ def tile_moe_two_lin_gelu_kernel(
         def gather_v(a, j, lo, hi):
             nc.vector.tensor_copy(
                 planes[a][:, SLOTS * j + lo : SLOTS * j + hi], rows[a][j][:].indirect(entries(offs_t, lo, hi))
+            )
+
+        def gather_pair(j, lo, hi):
+            nc.vector.tensor_copy(pairs[:, j // 2, lo:hi, j % 2], rows[0][j][:].indirect(entries(offs_t, lo, hi)))
+
+        def weave_pairs(lo, hi):
+            nc.vector.tensor_copy(
+                woven[0][:, lo:hi, :].rearrange("p s j -> p (s j)").bitcast(I32).rearrange("p (c i h) -> p c h i", i=4, h=2),
+                pairs[:].rearrange("p h s j -> p h (s j)").bitcast(I32)[:, :, lo:hi].rearrange("p h (c i) -> p c h i", i=4),
             )
 
         def gather_s(a, j, lo, hi):
@@ -141,24 +151,28 @@ def tile_moe_two_lin_gelu_kernel(
 
         for j in range(4):
             for lo, hi in ((0, CHUNK), (CHUNK, C)) if j == 3 else ((0, C),):
-                gather_v(0, j, lo, hi)
+                gather_pair(j, lo, hi)
             gather_s(0, j, C, SLOTS)
-        for step in (weave, quantize):
-            step(0, 0, CHUNK)
-            step(0, CHUNK, SLOTS)
+        weave_pairs(0, CHUNK)
+        weave_pairs(CHUNK, C)
+        weave(0, C, SLOTS)
+        quantize(0, 0, C)
+        quantize(0, C, SLOTS)
         for c in range(4):
             matmul(0, c)
         for j in range(2):
             gather_s(1, j, 0, SLOTS)
-        gather_v(1, 2, 0, 192)
+        gather_v(1, 2, 0, 256)
         gather_v(1, 3, 0, 128)
         gather_v(1, 3, 128, 256)
-        gather_s(1, 2, 192, 512)
+        gather_s(1, 2, 256, 512)
         gather_s(1, 3, 256, 384)
         gather_s(1, 3, 384, 512)
         for pair in range(2):
             for c in (2 * pair, 2 * pair + 1):
-                weave(1, CHUNK * c, CHUNK * (c + 1))
+                weave(1, CHUNK * c, min(CHUNK * (c + 1), 448))
+            if pair == 1:
+                weave(1, 448, SLOTS, nc.scalar.copy)
             for c in (2 * pair, 2 * pair + 1):
                 quantize(1, CHUNK * c, CHUNK * (c + 1))
                 finish(c)

@@ -80,8 +80,8 @@ def tile_moe_two_lin_gelu_kernel(
 
         def weave(a, lo, hi, copy=nc.vector.tensor_copy):
             copy(
-                woven[a][:, lo:hi, :].rearrange("p (c i) j -> p c j i", i=4),
-                planes[a][:].rearrange("p (j s) -> p j s", j=4)[:, :, lo:hi].rearrange("p j (c i) -> p c j i", i=4),
+                woven[a][:, lo:hi, :].rearrange("p (c i) j -> p c j i", i=8),
+                planes[a][:].rearrange("p (j s) -> p j s", j=4)[:, :, lo:hi].rearrange("p j (c i) -> p c j i", i=8),
             )
 
         def quantize(a, lo, hi):
@@ -176,12 +176,10 @@ def tile_moe_two_lin_gelu_kernel(
             for c in (2 * pair, 2 * pair + 1):
                 quantize(1, CHUNK * c, CHUNK * (c + 1))
                 finish(c)
-        times_gate(0, 128)
-        scatter_s(0, 128)
-        scatter_v(128, 256)
-        times_gate(256, 352)
-        scatter_s(256, 352)
-        scatter_v(352, 512)
+        scatter_v(0, 128)
+        times_gate(128, 320)
+        scatter_s(128, 320)
+        scatter_v(320, 512)
         for cols in (slice(0, T // 2), slice(T // 2, T)):
             nc.vector.tensor_tensor(out_t[:, cols], by_vector[:, cols], by_scalar[:, cols], ADD)
             nc.sync.dma_start(out=out[:, cols], in_=out_t[:, cols])

@@ -131,8 +131,9 @@ def tile_moe_two_lin_gelu_kernel(
             )
 
         nc.vector.memset(w_scales[:].rearrange("p a e n -> p (a e n)").bitcast(I32), 0)
+        load_row(0, 0)
         nc.sync.dma_start(out=offs_t[:], in_=offs)
-        for j in range(4):
+        for j in range(1, 4):
             load_row(0, j)
         for j in range(4):
             load_w_scales(0, w8_scales, j)

@@ -22,6 +22,7 @@ CHUNK = 128
 BANK = 512
 LIST_ROWS = 16
 WIDE = 2 * SLOTS
+PAIRED = 288
 
 
 def tile_moe_two_lin_gelu_kernel(
@@ -39,7 +40,7 @@ def tile_moe_two_lin_gelu_kernel(
             for a in range(2)
         ]
         planes = [keep.tile([P, 4 * SLOTS], BF16, name=f"planes{a}", align_bytes=64) for a in range(2)]
-        pairs = keep.tile([P, 2, C, 2], BF16, name="pairs", align_bytes=64)
+        pairs = keep.tile([P, 2, PAIRED, 2], BF16, name="pairs", align_bytes=64)
         woven = [keep.tile([P, SLOTS, 4], BF16, name=f"woven{a}", align_bytes=64) for a in range(2)]
         words = [keep.tile([P, SLOTS], U32, name=f"words{a}", align_bytes=64) for a in range(2)]
         scales = [keep.tile([P, SLOTS], U8, name=f"scales{a}", align_bytes=64) for a in range(2)]
@@ -151,12 +152,12 @@ def tile_moe_two_lin_gelu_kernel(
         nc.sync.dma_start(out=dst_t[:], in_=dst)
 
         for j in range(4):
-            for lo, hi in ((0, CHUNK), (CHUNK, C)) if j == 3 else ((0, C),):
+            for lo, hi in ((0, CHUNK), (CHUNK, PAIRED)) if j == 3 else ((0, PAIRED),):
                 gather_pair(j, lo, hi)
-            gather_s(0, j, C, SLOTS)
+            gather_s(0, j, PAIRED, SLOTS)
         weave_pairs(0, CHUNK)
-        weave_pairs(CHUNK, C)
-        weave(0, C, SLOTS)
+        weave_pairs(CHUNK, PAIRED)
+        weave(0, PAIRED, SLOTS)
         quantize(0, 0, C)
         quantize(0, C, SLOTS)
         for c in range(4):

import concourse.mybir as mybir

E, K, N, T, C = 2, 1024, 128, 640, 256
FLOPS = 2 * K * N * E * C

F32 = mybir.dt.float32
BF16 = mybir.dt.bfloat16
I32 = mybir.dt.int32
U32 = mybir.dt.uint32
U16 = mybir.dt.uint16
U8 = mybir.dt.uint8
FP8X4 = mybir.dt.float8_e4m3fn_x4
FP4X4 = mybir.dt.float4_e2m1fn_x4
GELU = mybir.ActivationFunctionType.Gelu_apprx_tanh
COPY = mybir.ActivationFunctionType.Copy
MULT = mybir.AluOpType.mult
ADD = mybir.AluOpType.add

P = 128
SLOTS = E * C
CHUNK = 128
BANK = 512
LIST_ROWS = 16
WIDE = 2 * SLOTS
PAIRED = 288


def tile_moe_two_lin_gelu_kernel(
    tc, xT, w8_words, w8_scales, w4_words, w4_scales, b, gate, offs, dst, out
):
    nc = tc.nc
    with (
        tc.tile_pool(name="keep", bufs=1) as keep,
        tc.psum_pool(name="psum", bufs=1) as psum,
    ):
        offs_t = keep.tile([P, SLOTS // LIST_ROWS], U16, name="offs_t")
        dst_t = keep.tile([P, SLOTS // LIST_ROWS], U16, name="dst_t")
        rows = [
            [keep.tile([P, WIDE if (a, j) in ((1, 0), (1, 1)) else T], F32, name=f"row{a}{j}", align_bytes=64) for j in range(4)]
            for a in range(2)
        ]
        planes = [keep.tile([P, 4 * SLOTS], BF16, name=f"planes{a}", align_bytes=64) for a in range(2)]
        pairs = keep.tile([P, 2, PAIRED, 2], BF16, name="pairs", align_bytes=64)
        woven = [keep.tile([P, SLOTS, 4], BF16, name=f"woven{a}", align_bytes=64) for a in range(2)]
        words = [keep.tile([P, SLOTS], U32, name=f"words{a}", align_bytes=64) for a in range(2)]
        scales = [keep.tile([P, SLOTS], U8, name=f"scales{a}", align_bytes=64) for a in range(2)]
        w8 = keep.tile([P, E, 4 * N], U8, name="w8", align_bytes=64)
        w4 = keep.tile([P, E, 2 * N], U8, name="w4", align_bytes=64)
        w_scales = keep.tile([P, 2, E, N], U8, name="w_scales", align_bytes=64)
        b_t = keep.tile([P, E], F32, name="b_t")
        gate_t = keep.tile([P, SLOTS], F32, name="gate_t")
        y = keep.tile([P, SLOTS], F32, name="y")
        gated = keep.tile([P, SLOTS], F32, name="gated")
        by_vector = keep.tile([P, T], F32, name="by_vector")
        by_scalar = keep.tile([P, T], F32, name="by_scalar")
        out_t = keep.tile([P, T], F32, name="out_t")
        warm = keep.tile([P, 1], F32, name="warm")
        acc = [psum.tile([P, BANK], F32, name=f"acc{c}") for c in range(SLOTS // CHUNK)]

        def entries(list_t, lo, hi):
            return list_t[:, lo // LIST_ROWS : hi // LIST_ROWS]

        def gather_v(a, j, lo, hi):
            nc.vector.tensor_copy(
                planes[a][:, SLOTS * j + lo : SLOTS * j + hi], rows[a][j][:].indirect(entries(offs_t, lo, hi))
            )

        def gather_pair(j, lo, hi):
            nc.vector.tensor_copy(pairs[:, j // 2, lo:hi, j % 2], rows[0][j][:].indirect(entries(offs_t, lo, hi)))

        def weave_pairs(lo, hi):
            nc.vector.tensor_copy(
                woven[0][:, lo:hi, :].rearrange("p s j -> p (s j)").bitcast(I32).rearrange("p (c i h) -> p c h i", i=4, h=2),
                pairs[:].rearrange("p h s j -> p h (s j)").bitcast(I32)[:, :, lo:hi].rearrange("p h (c i) -> p c h i", i=4),
            )

        def gather_s(a, j, lo, hi):
            nc.scalar.activation(
                planes[a][:, SLOTS * j + lo : SLOTS * j + hi], rows[a][j][:].indirect(entries(offs_t, lo, hi)), COPY
            )

        def weave(a, lo, hi, copy=nc.vector.tensor_copy):
            copy(
                woven[a][:, lo:hi, :].rearrange("p (c i) j -> p c j i", i=8),
                planes[a][:].rearrange("p (j s) -> p j s", j=4)[:, :, lo:hi].rearrange("p j (c i) -> p c j i", i=8),
            )

        def quantize(a, lo, hi):
            nc.vector.quantize_mx(
                out=words[a][:, lo:hi].bitcast(FP8X4),
                scales=scales[a][:, lo:hi],
                in_=woven[a][:, lo:hi, :].rearrange("p t j -> p (t j)"),
            )

        def matmul(a, c):
            e = CHUNK * c // C
            cols = slice(CHUNK * c, CHUNK * (c + 1))
            w = w8[:, e, :].bitcast(FP8X4) if a == 0 else w4[:, e, :].bitcast(FP4X4)
            nc.tensor.matmul_mx(
                out=acc[c][:, :CHUNK],
                lhsT=w,
                lhsT_scale=w_scales[:, a, e, :],
                rhs=words[a][:, cols].bitcast(FP8X4),
                rhs_scale=scales[a][:, cols],
                start=(a == 0),
                stop=(a == 1),
            )

        def finish(c):
            e = CHUNK * c // C
            matmul(1, c)
            nc.scalar.activation(y[:, CHUNK * c : CHUNK * (c + 1)], acc[c][:, :CHUNK], GELU, bias=b_t[:, e : e + 1])

        def times_gate(lo, hi):
            nc.vector.tensor_tensor(gated[:, lo:hi], y[:, lo:hi], gate_t[:, lo:hi], MULT)

        def scatter_s(lo, hi):
            nc.scalar.activation(by_scalar[:].indirect(entries(dst_t, lo, hi)), gated[:, lo:hi], COPY)

        def scatter_v(lo, hi):
            nc.vector.tensor_tensor(by_vector[:].indirect(entries(dst_t, lo, hi)), y[:, lo:hi], gate_t[:, lo:hi], MULT)

        def load_w_scales(a, src, g):
            nc.sync.dma_start(
                out=w_scales[32 * g : 32 * g + 4, a, :, :].bitcast(I32),
                in_=src[:, 0, 4 * g : 4 * g + 4, :].rearrange("e q n -> q e n").bitcast(I32),
            )

        def load_row(a, j):
            nc.sync.dma_start(
                out=rows[a][j][:, :T], in_=xT[4 * P * a : 4 * P * (a + 1), :].rearrange("(p j) t -> p j t", j=4)[:, j, :]
            )

        nc.vector.memset(w_scales[:].rearrange("p a e n -> p (a e n)").bitcast(I32), 0)
        load_row(0, 0)
        nc.sync.dma_start(out=offs_t[:], in_=offs)
        for j in range(1, 4):
            load_row(0, j)
        for j in range(4):
            load_w_scales(0, w8_scales, j)
            load_row(1, j)
        nc.vector.memset(warm[:], 0.0)
        nc.vector.memset(by_vector[:], 0.0)
        nc.vector.memset(by_scalar[:], 0.0)
        nc.scalar.activation(warm[:], warm[:], GELU)
        nc.sync.dma_start(out=w8[:].bitcast(I32), in_=w8_words[:, 0].rearrange("e p n r -> p e (n r)").bitcast(I32))
        for g in range(4):
            load_w_scales(1, w4_scales, g)
        nc.sync.dma_start(out=w4[:].bitcast(I32), in_=w4_words[:, 0].rearrange("e p x -> p e x").bitcast(I32))
        nc.sync.dma_start(out=gate_t[:], in_=gate)
        nc.sync.dma_start(out=b_t[:], in_=b)
        nc.sync.dma_start(out=dst_t[:], in_=dst)

        for j in range(4):
            for lo, hi in ((0, CHUNK), (CHUNK, PAIRED)) if j == 3 else ((0, PAIRED),):
                gather_pair(j, lo, hi)
            gather_s(0, j, PAIRED, SLOTS)
        weave_pairs(0, CHUNK)
        weave_pairs(CHUNK, PAIRED)
        weave(0, PAIRED, SLOTS)
        quantize(0, 0, C)
        quantize(0, C, SLOTS)
        for c in range(4):
            matmul(0, c)
        for j in range(2):
            gather_s(1, j, 0, SLOTS)
        gather_v(1, 2, 0, 256)
        gather_v(1, 3, 0, 128)
        gather_v(1, 3, 128, 256)
        gather_s(1, 2, 256, 512)
        gather_s(1, 3, 256, 384)
        gather_s(1, 3, 384, 512)
        for pair in range(2):
            for c in (2 * pair, 2 * pair + 1):
                weave(1, CHUNK * c, min(CHUNK * (c + 1), 448))
            if pair == 1:
                weave(1, 448, SLOTS, nc.scalar.copy)
            for c in (2 * pair, 2 * pair + 1):
                quantize(1, CHUNK * c, CHUNK * (c + 1))
                finish(c)
        scatter_v(0, 128)
        times_gate(128, 320)
        scatter_s(128, 320)
        scatter_v(320, 512)
        for cols in (slice(0, T // 2), slice(T // 2, T)):
            nc.vector.tensor_tensor(out_t[:, cols], by_vector[:, cols], by_scalar[:, cols], ADD)
            nc.sync.dma_start(out=out[:, cols], in_=out_t[:, cols])
